import numpy as np
import ml_dtypes


def mxq(x, axis, fmt="e4m3"):
    dtype, down = {"e4m3": (ml_dtypes.float8_e4m3fn, 7), "e5m2": (ml_dtypes.float8_e5m2, 14)}[fmt]
    v = np.moveaxis(np.asarray(x, np.float32).astype(ml_dtypes.bfloat16).astype(np.float64), axis, -1)
    blocks = v.reshape(v.shape[:-1] + (-1, 32))
    amax = np.abs(blocks).max(-1, keepdims=True)
    byte = np.maximum(np.where(amax > 0, np.frexp(amax)[1] - 1 + 127, 0) - down, 1)
    scale = np.exp2(byte - 127.0)
    codes = (blocks / scale).astype(np.float32).astype(dtype).astype(np.float64)
    return np.moveaxis((codes * scale).reshape(v.shape), -1, axis)


WIDE = False


def mx_kscale(k):
    if not WIDE:
        return np.ones(k)
    levels = np.array([10, -10, 5, -5, 0])
    if k % 512:
        return np.exp2(np.random.permutation(np.resize(levels, k // 32))).repeat(32)
    a = np.empty((k // 512, 16))
    for p in range(k // 512):
        a[p, :8] = np.random.permutation(np.resize(levels, 8))
        for g in range(8):
            far = levels[np.abs(levels - a[p, g]) >= 10]
            a[p, g + 8] = far[np.random.randint(len(far))]
    return np.exp2(a.ravel()).repeat(32)


def f64(x):
    return np.asarray(x).astype(np.float64)


def striped(idx):
    return np.tile(idx.reshape(-1, 16).T, (8, 1)).astype(np.uint16)


def unstriped(offs):
    return offs[:16].T.reshape(-1).astype(np.int64)


E2M1 = np.array([0.0, 0.5, 1.0, 1.5, 2.0, 3.0, 4.0, 6.0, -0.0, -0.5, -1.0, -1.5, -2.0, -3.0, -4.0, -6.0])


def pack_fp4(w):
    k, n = w.shape
    w = f64(np.asarray(w, np.float32).astype(ml_dtypes.bfloat16)).reshape(k // 32, 32, n)
    amax = np.abs(w).max(1)
    mant, ex = np.frexp(amax / 6.0)
    byte = np.clip(np.where(amax > 0, np.where(mant > 0.5, ex, ex - 1) + 127, 1), 1, 254)
    scaled = (w * np.exp2(127.0 - byte)[:, None, :]).reshape(k, n).astype(np.float32)
    c = np.ascontiguousarray(scaled.reshape(k // 512, 128, 4, n).transpose(0, 1, 3, 2)).astype(ml_dtypes.float4_e2m1fn).view(np.uint8) & 0xF
    words = (c[..., 0::2] | (c[..., 1::2] << 4)).reshape(k // 512, 128, 2 * n)
    return np.ascontiguousarray(words), np.ascontiguousarray(byte.astype(np.uint8).reshape(k // 512, 16, n))


def unpack_fp4(words, scales):
    g, _, n = scales.shape
    words = np.ascontiguousarray(words).reshape(g, 128, n, 2)
    nib = np.empty((g, 128, n, 4), np.uint8)
    nib[..., 0::2] = words & 0xF
    nib[..., 1::2] = words >> 4
    vals = E2M1[nib] * np.repeat(np.exp2(scales.astype(np.float64) - 127.0), 8, axis=1)[..., None]
    return vals.transpose(0, 1, 3, 2).reshape(g * 512, n)


def sigmoid(v):
    return 1.0 / (1.0 + np.exp(-np.maximum(v, -700.0)))


K, T, S, V, N = 512, 2048, 1024, 512, 256


def setup_inputs():
    n = np.random.standard_normal
    s = mx_kscale(K)[:, None]
    packed_xT = pack_fp4(n((K, T)) * s)
    return {
        "x_words": packed_xT[0],
        "x_scales": packed_xT[1],
        "w1": (n((K, N)) / np.sqrt(K) / s).astype(np.float32),
        "w2": (n((K, N)) / np.sqrt(K) / s).astype(np.float32),
        "w3": (n((K, N)) / np.sqrt(K) / s).astype(np.float32),
        "offs": striped(np.random.permutation(T)[:S]),
        "cen": striped(np.random.permutation(S)[:V]),
        "pos1": striped(np.random.permutation(S)[:V]),
        "pos2": striped(np.random.permutation(S)[:V]),
        "pos3": striped(np.random.permutation(S)[:V]),
        "pos4": striped(np.random.permutation(S)[:V]),
    }


def reference(x_words, x_scales, w1, w2, w3, offs, cen, pos1, pos2, pos3, pos4):
    xq = unpack_fp4(x_words, x_scales)[:, unstriped(offs)]
    y = mxq(f64(w1), 0, "e4m3").T @ xq
    yc = y[:, unstriped(cen)]
    e = mxq(f64(w2), 0, "e4m3").T @ xq
    h = mxq(f64(w3), 0, "e4m3").T @ xq
    z = (sigmoid(yc + e[:, unstriped(pos1)])) * h[:, unstriped(pos1)] + (sigmoid(yc + e[:, unstriped(pos2)])) * h[:, unstriped(pos2)] + (sigmoid(yc + e[:, unstriped(pos3)])) * h[:, unstriped(pos3)] + (sigmoid(yc + e[:, unstriped(pos4)])) * h[:, unstriped(pos4)]
    return z

@@ -1,0 +1,179 @@
+from contextlib import ExitStack
+
+import concourse.mybir as mybir
+from concourse.masks import make_identity
+
+K, T, S, V, N = 512, 2048, 1024, 512, 256
+FLOPS = 3 * 2 * K * N * S
+
+F32 = mybir.dt.float32
+BF16 = mybir.dt.bfloat16
+I32 = mybir.dt.int32
+U32 = mybir.dt.uint32
+U16 = mybir.dt.uint16
+U8 = mybir.dt.uint8
+FP8X4 = mybir.dt.float8_e4m3fn_x4
+FP4X4 = mybir.dt.float4_e2m1fn_x4
+ADD = mybir.AluOpType.add
+MULT = mybir.AluOpType.mult
+SIGMOID = mybir.ActivationFunctionType.Sigmoid
+
+P = 128
+PACK = 4
+HALF = 512
+BLOCKS = N // P
+D = 4
+
+
+def tile_picked_gatedg_none_p_kernel(
+    tc, x_words, x_scales, w1, w2, w3, offs, cen, pos1, pos2, pos3, pos4, out
+):
+    nc = tc.nc
+    with ExitStack() as ctx:
+        keep = ctx.enter_context(tc.tile_pool(name="keep", bufs=1))
+        mm_psum = ctx.enter_context(tc.psum_pool(name="mm_psum", bufs=4))
+        sum_psum = ctx.enter_context(tc.psum_pool(name="sum_psum", bufs=2))
+
+        def load_list(name, src):
+            tile = keep.tile(list(src.shape), U16, name=name)
+            nc.sync.dma_start(tile[:], src)
+            return tile
+
+        offs_sb = load_list("offs_sb", offs)
+
+        scales_sb = keep.tile([P, T], U8, name="scales_sb")
+        for q in range(4):
+            nc.sync.dma_start(
+                scales_sb[32 * q : 32 * q + 32, :].bitcast(I32),
+                x_scales[0, 4 * q : 4 * q + 4, :].bitcast(I32).partition_broadcast(8),
+            )
+        words_sb = keep.tile([P, T], U16, name="words_sb")
+        nc.sync.dma_start(words_sb[:].bitcast(I32), x_words[0].bitcast(I32))
+
+        raw = []
+        for i, w in enumerate((w1, w2, w3)):
+            tile = keep.tile([P, PACK, N], F32, name="raw%d" % i)
+            nc.sync.dma_start(tile[:], w.rearrange("(p j) c -> p j c", j=PACK))
+            raw.append(tile)
+            if i == 1:
+                cen_sb = load_list("cen_sb", cen)
+        pos_sb = [load_list("pos_sb%d" % d, p) for d, p in enumerate((pos1, pos2, pos3, pos4))]
+
+        ident = keep.tile([P, P], F32, name="ident")
+        make_identity(nc, ident[:])
+        warm = keep.tile([P, 1], F32, name="warm")
+        nc.scalar.activation(warm[:], ident[:, 0:1], SIGMOID)
+
+        picked_scales = keep.tile([P, S], U8, name="picked_scales", align_bytes=64)
+        nc.vector.tensor_copy(picked_scales[:], scales_sb[:].indirect(offs_sb[:]))
+        picked_words = {}
+
+        def pick_words(hf, pieces, tag):
+            tile = keep.tile([P, HALF], U16, name="picked_words%d" % hf, tag=tag, align_bytes=64)
+            width = HALF // pieces
+            for n in range(pieces):
+                first = hf * HALF + n * width
+                nc.vector.tensor_copy(
+                    tile[:, n * width : (n + 1) * width],
+                    words_sb[:].indirect(offs_sb[:, first // 16 : (first + width) // 16]),
+                )
+            picked_words[hf] = tile
+
+        codes = {}
+        planes = {}
+
+        def quantise(i, b):
+            grouped = keep.tile([P, P, PACK], BF16, name="grouped%d_%d" % (i, b), tag="grouped%d_%d" % (i, b), align_bytes=64)
+            nc.scalar.copy(
+                grouped[:].rearrange("p (c i) t -> p c t i", i=4),
+                raw[i][:, :, b * P : (b + 1) * P].rearrange("p t (c i) -> p c t i", i=4),
+            )
+            codes[i, b] = keep.tile([P, P], U32, name="codes%d_%d" % (i, b), align_bytes=64)
+            planes[i, b] = keep.tile([P, P], U8, name="planes%d_%d" % (i, b), align_bytes=64)
+            nc.vector.quantize_mx(
+                out=codes[i, b][:].bitcast(FP8X4),
+                scales=planes[i, b][:],
+                in_=grouped[:].rearrange("p c t -> p (c t)"),
+            )
+
+        rows = {}
+
+        def product(i, b, first, width):
+            if (i, b) not in rows:
+                rows[i, b] = keep.tile([P, S], F32, name="rows%d_%d" % (i, b))
+            acc = mm_psum.tile([P, HALF], F32, name="acc")
+            cols = slice(first, first + width)
+            hf, start = divmod(first, HALF)
+            nc.tensor.matmul_mx(
+                out=acc[:, 0:width],
+                lhsT=codes[i, b][:].bitcast(FP8X4),
+                lhsT_scale=planes[i, b][:],
+                rhs=picked_words[hf][:, start : start + width].bitcast(FP4X4),
+                rhs_scale=picked_scales[:, cols],
+                start=True,
+                stop=True,
+            )
+            nc.scalar.copy(rows[i, b][:, cols], acc[:, 0:width])
+
+        pick_words(0, 1, "picked_words0")
+        quantise(0, 0)
+        pick_words(1, 2, "grouped0_0")
+        product(0, 0, 0, HALF)
+        quantise(1, 0)
+        product(0, 0, HALF, HALF // 2)
+        product(0, 0, HALF + HALF // 2, HALF // 2)
+        for hf in range(2):
+            product(1, 0, hf * HALF, HALF)
+        quantise(0, 1)
+        quantise(1, 1)
+        quantise(2, 0)
+        for hf in range(2):
+            product(2, 0, hf * HALF, HALF)
+        quantise(2, 1)
+
+        def pe_sum(terms, b):
+            turned_ps = sum_psum.tile([P, V], F32, name="turned_ps")
+            for c in range(V // P):
+                cols = slice(c * P, (c + 1) * P)
+                for n, term in enumerate(terms):
+                    nc.tensor.matmul(
+                        turned_ps[:, cols], term[:, cols], ident[:], is_transpose=True,
+                        start=(n == 0), stop=(n == len(terms) - 1),
+                    )
+            turned = keep.tile([P, V], F32, name="turned%d" % b)
+            nc.scalar.copy(turned[:], turned_ps[:])
+            back_ps = sum_psum.tile([P, V], F32, name="back_ps")
+            for c in range(V // P):
+                cols = slice(c * P, (c + 1) * P)
+                nc.tensor.transpose(back_ps[:, cols], turned[:, cols], ident[:])
+            return back_ps
+
+        for b in range(BLOCKS):
+            centre = keep.tile([P, V], F32, name="centre%d" % b)
+            nc.vector.tensor_copy(centre[:], rows[0, b][:].indirect(cen_sb[:]))
+            gates = []
+            for d in range(D):
+                pre = keep.tile([P, V], F32, name="pre%d_%d" % (b, d))
+                nc.vector.tensor_tensor(pre[:], rows[1, b][:].indirect(pos_sb[d][:]), centre[:], ADD)
+                gate = keep.tile([P, V], F32, name="gate%d_%d" % (b, d))
+                nc.scalar.activation(gate[:], pre[:], SIGMOID)
+                gates.append(gate)
+            if b == 0:
+                for i in range(3):
+                    for hf in range(2):
+                        product(i, 1, hf * HALF, HALF)
+            terms = []
+            result = keep.tile([P, V], F32, name="result%d" % b)
+            for d in range(D):
+                term = keep.tile([P, V], F32, name="term%d_%d" % (b, d))
+                nc.vector.tensor_tensor(term[:], rows[2, b][:].indirect(pos_sb[d][:]), gates[d][:], MULT)
+                terms.append(term)
+                if b == 1 and d == 1:
+                    first_two = pe_sum(terms, b)
+            if b == 0:
+                nc.scalar.copy(result[:], pe_sum(terms, b)[:])
+            else:
+                three = keep.tile([P, V], F32, name="three")
+                nc.vector.tensor_tensor(three[:], first_two[:], terms[2][:], ADD)
+                nc.vector.tensor_tensor(result[:], three[:], terms[3][:], ADD)
+            nc.sync.dma_start(out[b * P : (b + 1) * P, :], result[:])

@@ -32,7 +32,7 @@ def tile_picked_gatedg_none_p_kernel(
     with ExitStack() as ctx:
         keep = ctx.enter_context(tc.tile_pool(name="keep", bufs=1))
         mm_psum = ctx.enter_context(tc.psum_pool(name="mm_psum", bufs=4))
-        sum_psum = ctx.enter_context(tc.psum_pool(name="sum_psum", bufs=2))
+        sum_psum = ctx.enter_context(tc.psum_pool(name="sum_psum", bufs=1))
 
         def load_list(name, src):
             tile = keep.tile(list(src.shape), U16, name=name)
@@ -117,63 +117,102 @@ def tile_picked_gatedg_none_p_kernel(
 
         pick_words(0, 1, "picked_words0")
         quantise(0, 0)
+        quantise(0, 1)
         pick_words(1, 2, "grouped0_0")
         product(0, 0, 0, HALF)
         quantise(1, 0)
+        quantise(1, 1)
         product(0, 0, HALF, HALF // 2)
         product(0, 0, HALF + HALF // 2, HALF // 2)
-        for hf in range(2):
-            product(1, 0, hf * HALF, HALF)
-        quantise(0, 1)
-        quantise(1, 1)
-        quantise(2, 0)
-        for hf in range(2):
-            product(2, 0, hf * HALF, HALF)
-        quantise(2, 1)
+        for i, b in ((0, 1), (1, 0)):
+            for hf in range(2):
+                product(i, b, hf * HALF, HALF)
 
-        def pe_sum(terms, b):
-            turned_ps = sum_psum.tile([P, V], F32, name="turned_ps")
-            for c in range(V // P):
-                cols = slice(c * P, (c + 1) * P)
-                for n, term in enumerate(terms):
-                    nc.tensor.matmul(
-                        turned_ps[:, cols], term[:, cols], ident[:], is_transpose=True,
-                        start=(n == 0), stop=(n == len(terms) - 1),
-                    )
-            turned = keep.tile([P, V], F32, name="turned%d" % b)
-            nc.scalar.copy(turned[:], turned_ps[:])
-            back_ps = sum_psum.tile([P, V], F32, name="back_ps")
-            for c in range(V // P):
-                cols = slice(c * P, (c + 1) * P)
-                nc.tensor.transpose(back_ps[:, cols], turned[:, cols], ident[:])
-            return back_ps
-
+        centres = []
         for b in range(BLOCKS):
             centre = keep.tile([P, V], F32, name="centre%d" % b)
             nc.vector.tensor_copy(centre[:], rows[0, b][:].indirect(cen_sb[:]))
-            gates = []
-            for d in range(D):
-                pre = keep.tile([P, V], F32, name="pre%d_%d" % (b, d))
-                nc.vector.tensor_tensor(pre[:], rows[1, b][:].indirect(pos_sb[d][:]), centre[:], ADD)
-                gate = keep.tile([P, V], F32, name="gate%d_%d" % (b, d))
-                nc.scalar.activation(gate[:], pre[:], SIGMOID)
-                gates.append(gate)
-            if b == 0:
-                for i in range(3):
-                    for hf in range(2):
-                        product(i, 1, hf * HALF, HALF)
-            terms = []
-            result = keep.tile([P, V], F32, name="result%d" % b)
-            for d in range(D):
-                term = keep.tile([P, V], F32, name="term%d_%d" % (b, d))
-                nc.vector.tensor_tensor(term[:], rows[2, b][:].indirect(pos_sb[d][:]), gates[d][:], MULT)
-                terms.append(term)
-                if b == 1 and d == 1:
-                    first_two = pe_sum(terms, b)
-            if b == 0:
-                nc.scalar.copy(result[:], pe_sum(terms, b)[:])
+            centres.append(centre)
+
+        quantise(2, 0)
+        quantise(2, 1)
+        for hf in range(2):
+            product(1, 1, hf * HALF, HALF)
+
+        W = V // 2
+        gates = {}
+
+        def gate(b, d):
+            pre = keep.tile([P, V], F32, name="pre%d_%d" % (b, d))
+            nc.vector.tensor_tensor(pre[:], rows[1, b][:].indirect(pos_sb[d][:]), centres[b][:], ADD)
+            if d < D - 1:
+                gates[b, d] = keep.tile([P, V], F32, name="gate%d_%d" % (b, d))
+                nc.scalar.activation(gates[b, d][:], pre[:], SIGMOID)
             else:
-                three = keep.tile([P, V], F32, name="three")
-                nc.vector.tensor_tensor(three[:], first_two[:], terms[2][:], ADD)
-                nc.vector.tensor_tensor(result[:], three[:], terms[3][:], ADD)
-            nc.sync.dma_start(out[b * P : (b + 1) * P, :], result[:])
+                for u in range(2):
+                    name = "gate%d_%d_%d" % (b, d, u)
+                    gates[b, d, u] = keep.tile([P, W], F32, name=name, tag=name)
+                    nc.scalar.activation(gates[b, d, u][:], pre[:, u * W : (u + 1) * W], SIGMOID)
+
+        def term(b, d):
+            tile = keep.tile([P, V], F32, name="term%d_%d" % (b, d))
+            nc.vector.tensor_tensor(tile[:], rows[2, b][:].indirect(pos_sb[d][:]), gates[b, d][:], MULT)
+            return tile
+
+        def last_term(b, u, tag):
+            tile = keep.tile([P, W], F32, name="last%d_%d" % (b, u), tag=tag)
+            nc.vector.tensor_tensor(
+                tile[:], rows[2, b][:].indirect(pos_sb[D - 1][:, u * W // 16 : (u + 1) * W // 16]), gates[b, D - 1, u][:], MULT
+            )
+            return tile
+
+        def add_turned(acc, src, first, last):
+            chunks = src.shape[1] // P
+            for c in range(chunks):
+                cols = slice(c * P, (c + 1) * P)
+                nc.tensor.matmul(
+                    acc[:, cols], src[:, cols], ident[:], is_transpose=True,
+                    start=(first and c == 0), stop=(last and c == chunks - 1),
+                )
+
+        def turn_back(acc, name):
+            width = acc.shape[1]
+            turned = keep.tile([P, width], F32, name=name)
+            nc.scalar.copy(turned[:], acc)
+            back = mm_psum.tile([P, HALF], F32, name="acc")
+            for c in range(width // P):
+                cols = slice(c * P, (c + 1) * P)
+                nc.tensor.transpose(back[:, cols], turned[:, cols], ident[:])
+            return back
+
+        for d in range(D):
+            gate(0, d)
+            if d < 2:
+                product(2, 0, d * HALF, HALF)
+        for d in range(D):
+            gate(1, d)
+            if d < 2:
+                product(2, 1, d * HALF, HALF)
+
+        sum0 = sum_psum.tile([P, V], F32, name="sum0")
+        for d in range(D - 1):
+            add_turned(sum0[:], term(0, d)[:], d == 0, d == D - 2)
+        partial0 = turn_back(sum0[:], "turned0")
+
+        sum1 = [sum_psum.tile([P, W], F32, name="sum1_%d" % u) for u in range(2)]
+        for d in range(D - 1):
+            tile = term(1, d)
+            for u in range(2):
+                add_turned(sum1[u][:], tile[:, u * W : (u + 1) * W], d == 0, False)
+        for u in range(2):
+            add_turned(sum1[u][:], last_term(1, u, "last1_%d" % u)[:], False, True)
+            back = turn_back(sum1[u][:], "turned1_%d" % u)
+            result = keep.tile([P, W], F32, name="result1_%d" % u)
+            nc.scalar.copy(result[:], back[:, 0:W])
+            nc.sync.dma_start(out[P : 2 * P, u * W : (u + 1) * W], result[:])
+
+        lasts = [last_term(0, u, "gate1_%d_%d" % (D - 1, u)) for u in range(2)]
+        for u in range(2):
+            result = keep.tile([P, W], F32, name="result0_%d" % u)
+            nc.vector.tensor_tensor(result[:], partial0[:, u * W : (u + 1) * W], lasts[u][:], ADD)
+            nc.sync.dma_start(out[0:P, u * W : (u + 1) * W], result[:])

@@ -16,6 +16,7 @@ FP8X4 = mybir.dt.float8_e4m3fn_x4
 FP4X4 = mybir.dt.float4_e2m1fn_x4
 ADD = mybir.AluOpType.add
 MULT = mybir.AluOpType.mult
+COPY = mybir.ActivationFunctionType.Copy
 SIGMOID = mybir.ActivationFunctionType.Sigmoid
 
 P = 128
@@ -31,7 +32,7 @@ def tile_picked_gatedg_none_p_kernel(
     nc = tc.nc
     with ExitStack() as ctx:
         keep = ctx.enter_context(tc.tile_pool(name="keep", bufs=1))
-        mm_psum = ctx.enter_context(tc.psum_pool(name="mm_psum", bufs=4))
+        mm_psum = ctx.enter_context(tc.psum_pool(name="mm_psum", bufs=3))
         sum_psum = ctx.enter_context(tc.psum_pool(name="sum_psum", bufs=1))
 
         def load_list(name, src):
@@ -42,30 +43,36 @@ def tile_picked_gatedg_none_p_kernel(
         offs_sb = load_list("offs_sb", offs)
 
         scales_sb = keep.tile([P, T], U8, name="scales_sb")
+        nc.gpsimd.memset(scales_sb[:].bitcast(I32), 0)
         for q in range(4):
             nc.sync.dma_start(
-                scales_sb[32 * q : 32 * q + 32, :].bitcast(I32),
-                x_scales[0, 4 * q : 4 * q + 4, :].bitcast(I32).partition_broadcast(8),
+                scales_sb[32 * q : 32 * q + 4, :].bitcast(I32), x_scales[0, 4 * q : 4 * q + 4, :].bitcast(I32)
             )
         words_sb = keep.tile([P, T], U16, name="words_sb")
         nc.sync.dma_start(words_sb[:].bitcast(I32), x_words[0].bitcast(I32))
 
-        raw = []
-        for i, w in enumerate((w1, w2, w3)):
-            tile = keep.tile([P, PACK, N], F32, name="raw%d" % i)
-            nc.sync.dma_start(tile[:], w.rearrange("(p j) c -> p j c", j=PACK))
-            raw.append(tile)
-            if i == 1:
-                cen_sb = load_list("cen_sb", cen)
+        raw = {}
+
+        def load_block(i, w, b):
+            name = "raw%d_%d" % (i, b)
+            tile = keep.tile([P, PACK, P], F32, name=name, tag=name, align_bytes=64)
+            nc.sync.dma_start(tile[:], w[:, b * P : (b + 1) * P].rearrange("(p j) c -> p j c", j=PACK))
+            raw[i, b] = tile[:]
+
+        load_block(0, w1, 0)
+        load_block(1, w2, 0)
+        load_block(2, w3, 0)
+        load_block(0, w1, 1)
+        cen_sb = load_list("cen_sb", cen)
         pos_sb = [load_list("pos_sb%d" % d, p) for d, p in enumerate((pos1, pos2, pos3, pos4))]
+        load_block(1, w2, 1)
+        load_block(2, w3, 1)
 
         ident = keep.tile([P, P], F32, name="ident")
         make_identity(nc, ident[:])
         warm = keep.tile([P, 1], F32, name="warm")
         nc.scalar.activation(warm[:], ident[:, 0:1], SIGMOID)
 
-        picked_scales = keep.tile([P, S], U8, name="picked_scales", align_bytes=64)
-        nc.vector.tensor_copy(picked_scales[:], scales_sb[:].indirect(offs_sb[:]))
         picked_words = {}
 
         def pick_words(hf, pieces, tag):
@@ -82,77 +89,120 @@ def tile_picked_gatedg_none_p_kernel(
         codes = {}
         planes = {}
 
-        def quantise(i, b):
-            grouped = keep.tile([P, P, PACK], BF16, name="grouped%d_%d" % (i, b), tag="grouped%d_%d" % (i, b), align_bytes=64)
-            nc.scalar.copy(
-                grouped[:].rearrange("p (c i) t -> p c t i", i=4),
-                raw[i][:, :, b * P : (b + 1) * P].rearrange("p t (c i) -> p c t i", i=4),
-            )
-            codes[i, b] = keep.tile([P, P], U32, name="codes%d_%d" % (i, b), align_bytes=64)
-            planes[i, b] = keep.tile([P, P], U8, name="planes%d_%d" % (i, b), align_bytes=64)
+        def quantise(parts, tag):
+            name = "%d_%d" % parts[0]
+            width = len(parts) * P
+            grouped = keep.tile([P, width, PACK], BF16, name="grouped" + name, tag=tag, align_bytes=64)
+            words = keep.tile([P, width], U32, name="codes" + name, tag="codes" + name, align_bytes=64)
+            plane = keep.tile([P, width], U8, name="planes" + name, align_bytes=64)
+            for n, part in enumerate(parts):
+                cols = slice(n * P, (n + 1) * P)
+                nc.scalar.copy(
+                    grouped[:, cols, :].rearrange("p (c i) t -> p c t i", i=4),
+                    raw[part].rearrange("p t (c i) -> p c t i", i=4),
+                )
+                codes[part] = words[:, cols]
+                planes[part] = plane[:, cols]
             nc.vector.quantize_mx(
-                out=codes[i, b][:].bitcast(FP8X4),
-                scales=planes[i, b][:],
-                in_=grouped[:].rearrange("p c t -> p (c t)"),
+                out=words[:].bitcast(FP8X4), scales=plane[:], in_=grouped[:].rearrange("p c t -> p (c t)")
             )
 
         rows = {}
 
-        def product(i, b, first, width):
-            if (i, b) not in rows:
-                rows[i, b] = keep.tile([P, S], F32, name="rows%d_%d" % (i, b))
+        def multiply(i, b, first, width):
             acc = mm_psum.tile([P, HALF], F32, name="acc")
             cols = slice(first, first + width)
             hf, start = divmod(first, HALF)
             nc.tensor.matmul_mx(
                 out=acc[:, 0:width],
-                lhsT=codes[i, b][:].bitcast(FP8X4),
-                lhsT_scale=planes[i, b][:],
+                lhsT=codes[i, b].bitcast(FP8X4),
+                lhsT_scale=planes[i, b],
                 rhs=picked_words[hf][:, start : start + width].bitcast(FP4X4),
                 rhs_scale=picked_scales[:, cols],
                 start=True,
                 stop=True,
             )
-            nc.scalar.copy(rows[i, b][:, cols], acc[:, 0:width])
+            return acc
+
+        def empty(acc, i, b, first, width):
+            if (i, b) not in rows:
+                rows[i, b] = keep.tile([P, S], F32, name="rows%d_%d" % (i, b), tag="raw0_1" if (i, b) == (0, 0) else "rows%d_%d" % (i, b), align_bytes=64)
+            nc.scalar.copy(rows[i, b][:, first : first + width], acc[:, 0:width])
+
+        def product(i, b, first, width):
+            empty(multiply(i, b, first, width), i, b, first, width)
 
         pick_words(0, 1, "picked_words0")
-        quantise(0, 0)
-        quantise(0, 1)
-        pick_words(1, 2, "grouped0_0")
+        picked_scales = keep.tile([P, S], U8, name="picked_scales", align_bytes=64)
+        nc.vector.tensor_copy(picked_scales[:], scales_sb[:].indirect(offs_sb[:]))
+        quantise([(0, 0), (1, 0)], "grouped0_0")
+        pick_words(1, 2, "raw1_0")
+        quantise([(2, 0), (0, 1)], "grouped2_0")
         product(0, 0, 0, HALF)
-        quantise(1, 0)
-        quantise(1, 1)
         product(0, 0, HALF, HALF // 2)
         product(0, 0, HALF + HALF // 2, HALF // 2)
-        for i, b in ((0, 1), (1, 0)):
-            for hf in range(2):
-                product(i, b, hf * HALF, HALF)
-
-        centres = []
-        for b in range(BLOCKS):
-            centre = keep.tile([P, V], F32, name="centre%d" % b)
-            nc.vector.tensor_copy(centre[:], rows[0, b][:].indirect(cen_sb[:]))
-            centres.append(centre)
-
-        quantise(2, 0)
-        quantise(2, 1)
         for hf in range(2):
-            product(1, 1, hf * HALF, HALF)
+            product(1, 0, hf * HALF, HALF)
+
+        centres = {}
+
+        def centre(b, pieces):
+            centres[b] = keep.tile([P, V], F32, name="centre%d" % b)
+            width = V // pieces
+            for n in range(pieces):
+                nc.vector.tensor_copy(
+                    centres[b][:, n * width : (n + 1) * width],
+                    rows[0, b][:].indirect(cen_sb[:, n * width // 16 : (n + 1) * width // 16]),
+                )
+
+        centre(0, 2)
 
         W = V // 2
         gates = {}
 
-        def gate(b, d):
-            pre = keep.tile([P, V], F32, name="pre%d_%d" % (b, d))
-            nc.vector.tensor_tensor(pre[:], rows[1, b][:].indirect(pos_sb[d][:]), centres[b][:], ADD)
+        def add_turned(acc, src, first, last):
+            chunks = src.shape[1] // P
+            for c in range(chunks):
+                cols = slice(c * P, (c + 1) * P)
+                nc.tensor.matmul(
+                    acc[:, cols], src[:, cols], ident[:], is_transpose=True,
+                    start=(first and c == 0), stop=(last and c == chunks - 1),
+                )
+
+        def leave(acc, name, func):
+            turned = keep.tile([P, acc.shape[1]], F32, name=name)
+            nc.scalar.activation(turned[:], acc, func)
+            return turned
+
+        def turn_back(turned):
+            back = mm_psum.tile([P, HALF], F32, name="acc")
+            for c in range(turned.shape[1] // P):
+                cols = slice(c * P, (c + 1) * P)
+                nc.tensor.transpose(back[:, cols], turned[:, cols], ident[:])
+            return back
+
+        def write_gate(b, d, src, func):
             if d < D - 1:
                 gates[b, d] = keep.tile([P, V], F32, name="gate%d_%d" % (b, d))
-                nc.scalar.activation(gates[b, d][:], pre[:], SIGMOID)
+                nc.scalar.activation(gates[b, d][:], src[:], func)
             else:
                 for u in range(2):
                     name = "gate%d_%d_%d" % (b, d, u)
                     gates[b, d, u] = keep.tile([P, W], F32, name=name, tag=name)
-                    nc.scalar.activation(gates[b, d, u][:], pre[:, u * W : (u + 1) * W], SIGMOID)
+                    nc.scalar.activation(gates[b, d, u][:], src[:, u * W : (u + 1) * W], func)
+
+        def gate(b, d, pieces=1):
+            pre = keep.tile([P, V], F32, name="pre%d_%d" % (b, d))
+            width = V // pieces
+            for n in range(pieces):
+                cols = slice(n * width, (n + 1) * width)
+                nc.vector.tensor_tensor(
+                    pre[:, cols],
+                    rows[1, b][:].indirect(pos_sb[d][:, n * width // 16 : (n + 1) * width // 16]),
+                    centres[b][:, cols],
+                    ADD,
+                )
+            write_gate(b, d, pre, SIGMOID)
 
         def term(b, d):
             tile = keep.tile([P, V], F32, name="term%d_%d" % (b, d))
@@ -166,53 +216,46 @@ def tile_picked_gatedg_none_p_kernel(
             )
             return tile
 
-        def add_turned(acc, src, first, last):
-            chunks = src.shape[1] // P
-            for c in range(chunks):
-                cols = slice(c * P, (c + 1) * P)
-                nc.tensor.matmul(
-                    acc[:, cols], src[:, cols], ident[:], is_transpose=True,
-                    start=(first and c == 0), stop=(last and c == chunks - 1),
-                )
-
-        def turn_back(acc, name):
-            width = acc.shape[1]
-            turned = keep.tile([P, width], F32, name=name)
-            nc.scalar.copy(turned[:], acc)
-            back = mm_psum.tile([P, HALF], F32, name="acc")
-            for c in range(width // P):
-                cols = slice(c * P, (c + 1) * P)
-                nc.tensor.transpose(back[:, cols], turned[:, cols], ident[:])
-            return back
-
-        for d in range(D):
-            gate(0, d)
-            if d < 2:
-                product(2, 0, d * HALF, HALF)
-        for d in range(D):
-            gate(1, d)
-            if d < 2:
-                product(2, 1, d * HALF, HALF)
+        for hf in range(2):
+            product(2, 0, hf * HALF, HALF)
+        quantise([(1, 1), (2, 1)], "raw0_1")
+        gate(0, 0, 2)
+        gate(0, 1)
+        for hf in range(2):
+            product(0, 1, hf * HALF, HALF)
+        gate(0, 2)
+        gate(0, 3)
+        for i in (1, 2):
+            for hf in range(2):
+                product(i, 1, hf * HALF, HALF)
 
         sum0 = sum_psum.tile([P, V], F32, name="sum0")
         for d in range(D - 1):
+            if d == D - 2:
+                centre(1, 1)
             add_turned(sum0[:], term(0, d)[:], d == 0, d == D - 2)
-        partial0 = turn_back(sum0[:], "turned0")
+        for d in range(D):
+            gate(1, d)
+        partial0 = turn_back(leave(sum0[:], "turned0", COPY)[:])
 
         sum1 = [sum_psum.tile([P, W], F32, name="sum1_%d" % u) for u in range(2)]
         for d in range(D - 1):
             tile = term(1, d)
-            for u in range(2):
-                add_turned(sum1[u][:], tile[:, u * W : (u + 1) * W], d == 0, False)
-        for u in range(2):
-            add_turned(sum1[u][:], last_term(1, u, "last1_%d" % u)[:], False, True)
-            back = turn_back(sum1[u][:], "turned1_%d" % u)
-            result = keep.tile([P, W], F32, name="result1_%d" % u)
-            nc.scalar.copy(result[:], back[:, 0:W])
-            nc.sync.dma_start(out[P : 2 * P, u * W : (u + 1) * W], result[:])
+            for u in (1, 0):
+                add_turned(sum1[u][:], tile[:, u * W : (u + 1) * W], d == 0, u == 1 and d == D - 2)
+        partial1 = turn_back(leave(sum1[1][:], "turned1_1", COPY)[:])
+        add_turned(sum1[0][:], last_term(1, 0, "last1_0")[:], False, True)
+        back = turn_back(leave(sum1[0][:], "turned1_0", COPY)[:])
+        result = keep.tile([P, W], F32, name="result1_0")
+        nc.scalar.copy(result[:], back[:, 0:W])
+        nc.sync.dma_start(out[P : 2 * P, 0:W], result[:])
 
-        lasts = [last_term(0, u, "gate1_%d_%d" % (D - 1, u)) for u in range(2)]
-        for u in range(2):
-            result = keep.tile([P, W], F32, name="result0_%d" % u)
-            nc.vector.tensor_tensor(result[:], partial0[:, u * W : (u + 1) * W], lasts[u][:], ADD)
-            nc.sync.dma_start(out[0:P, u * W : (u + 1) * W], result[:])
+        closing = [
+            (1, 1, partial1[:, 0:W], last_term(1, 1, "last1_1")),
+            (0, 0, partial0[:, 0:W], last_term(0, 0, "gate1_3_0")),
+            (0, 1, partial0[:, W:V], last_term(0, 1, "gate1_3_1")),
+        ]
+        for b, u, partial, last in closing:
+            result = keep.tile([P, W], F32, name="result%d_%d" % (b, u))
+            nc.vector.tensor_tensor(result[:], partial, last[:], ADD)
+            nc.sync.dma_start(out[b * P : (b + 1) * P, u * W : (u + 1) * W], result[:])

@@ -32,7 +32,7 @@ def tile_picked_gatedg_none_p_kernel(
     nc = tc.nc
     with ExitStack() as ctx:
         keep = ctx.enter_context(tc.tile_pool(name="keep", bufs=1))
-        mm_psum = ctx.enter_context(tc.psum_pool(name="mm_psum", bufs=3))
+        mm_psum = ctx.enter_context(tc.psum_pool(name="mm_psum", bufs=5))
         sum_psum = ctx.enter_context(tc.psum_pool(name="sum_psum", bufs=1))
 
         def load_list(name, src):
@@ -60,9 +60,9 @@ def tile_picked_gatedg_none_p_kernel(
             raw[i, b] = tile[:]
 
         load_block(0, w1, 0)
+        load_block(0, w1, 1)
         load_block(1, w2, 0)
         load_block(2, w3, 0)
-        load_block(0, w1, 1)
         cen_sb = load_list("cen_sb", cen)
         pos_sb = [load_list("pos_sb%d" % d, p) for d, p in enumerate((pos1, pos2, pos3, pos4))]
         load_block(1, w2, 1)
@@ -126,7 +126,7 @@ def tile_picked_gatedg_none_p_kernel(
 
         def empty(acc, i, b, first, width):
             if (i, b) not in rows:
-                rows[i, b] = keep.tile([P, S], F32, name="rows%d_%d" % (i, b), tag="raw0_1" if (i, b) == (0, 0) else "rows%d_%d" % (i, b), align_bytes=64)
+                rows[i, b] = keep.tile([P, S], F32, name="rows%d_%d" % (i, b), tag="raw2_0" if (i, b) == (0, 0) else "rows%d_%d" % (i, b), align_bytes=64)
             nc.scalar.copy(rows[i, b][:, first : first + width], acc[:, 0:width])
 
         def product(i, b, first, width):
@@ -135,14 +135,15 @@ def tile_picked_gatedg_none_p_kernel(
         pick_words(0, 1, "picked_words0")
         picked_scales = keep.tile([P, S], U8, name="picked_scales", align_bytes=64)
         nc.vector.tensor_copy(picked_scales[:], scales_sb[:].indirect(offs_sb[:]))
-        quantise([(0, 0), (1, 0)], "grouped0_0")
-        pick_words(1, 2, "raw1_0")
-        quantise([(2, 0), (0, 1)], "grouped2_0")
+        quantise([(0, 0), (0, 1)], "grouped0_0")
+        pick_words(1, 2, "raw0_1")
+        quantise([(1, 0), (2, 0)], "grouped1_0")
         product(0, 0, 0, HALF)
         product(0, 0, HALF, HALF // 2)
         product(0, 0, HALF + HALF // 2, HALF // 2)
-        for hf in range(2):
-            product(1, 0, hf * HALF, HALF)
+        for i, b in ((0, 1), (1, 0)):
+            for hf in range(2):
+                product(i, b, hf * HALF, HALF)
 
         centres = {}
 
@@ -155,7 +156,8 @@ def tile_picked_gatedg_none_p_kernel(
                     rows[0, b][:].indirect(cen_sb[:, n * width // 16 : (n + 1) * width // 16]),
                 )
 
-        centre(0, 2)
+        centre(0, 1)
+        centre(1, 1)
 
         W = V // 2
         gates = {}
@@ -218,21 +220,15 @@ def tile_picked_gatedg_none_p_kernel(
 
         for hf in range(2):
             product(2, 0, hf * HALF, HALF)
-        quantise([(1, 1), (2, 1)], "raw0_1")
-        gate(0, 0, 2)
-        gate(0, 1)
-        for hf in range(2):
-            product(0, 1, hf * HALF, HALF)
-        gate(0, 2)
-        gate(0, 3)
+        quantise([(1, 1), (2, 1)], "raw2_0")
+        for d in range(D):
+            gate(0, d)
         for i in (1, 2):
             for hf in range(2):
                 product(i, 1, hf * HALF, HALF)
 
         sum0 = sum_psum.tile([P, V], F32, name="sum0")
         for d in range(D - 1):
-            if d == D - 2:
-                centre(1, 1)
             add_turned(sum0[:], term(0, d)[:], d == 0, d == D - 2)
         for d in range(D):
             gate(1, d)

@@ -184,8 +184,9 @@ def tile_picked_gatedg_none_p_kernel(
             return back
 
         def write_gate(b, d, src, func):
-            if d < D - 1:
-                gates[b, d] = keep.tile([P, V], F32, name="gate%d_%d" % (b, d))
+            if (b, d) != (1, D - 1):
+                name = "gate%d_%d" % (b, d)
+                gates[b, d] = keep.tile([P, V], F32, name=name, tag=name)
                 nc.scalar.activation(gates[b, d][:], src[:], func)
             else:
                 for u in range(2):
@@ -206,8 +207,9 @@ def tile_picked_gatedg_none_p_kernel(
                 )
             write_gate(b, d, pre, SIGMOID)
 
-        def term(b, d):
-            tile = keep.tile([P, V], F32, name="term%d_%d" % (b, d))
+        def term(b, d, tag=None):
+            name = "term%d_%d" % (b, d)
+            tile = keep.tile([P, V], F32, name=name, tag=tag or name)
             nc.vector.tensor_tensor(tile[:], rows[2, b][:].indirect(pos_sb[d][:]), gates[b, d][:], MULT)
             return tile
 
@@ -218,9 +220,9 @@ def tile_picked_gatedg_none_p_kernel(
             )
             return tile
 
+        quantise([(1, 1), (2, 1)], "raw2_0")
         for hf in range(2):
             product(2, 0, hf * HALF, HALF)
-        quantise([(1, 1), (2, 1)], "raw2_0")
         for d in range(D):
             gate(0, d)
         for i in (1, 2):
@@ -246,12 +248,14 @@ def tile_picked_gatedg_none_p_kernel(
         nc.scalar.copy(result[:], back[:, 0:W])
         nc.sync.dma_start(out[P : 2 * P, 0:W], result[:])
 
+        last0 = term(0, D - 1, "gate1_1")
+        last1 = last_term(1, 1, "last1_1")
         closing = [
-            (1, 1, partial1[:, 0:W], last_term(1, 1, "last1_1")),
-            (0, 0, partial0[:, 0:W], last_term(0, 0, "gate1_3_0")),
-            (0, 1, partial0[:, W:V], last_term(0, 1, "gate1_3_1")),
+            (0, 0, partial0[:, 0:W], last0[:, 0:W]),
+            (0, 1, partial0[:, W:V], last0[:, W:V]),
+            (1, 1, partial1[:, 0:W], last1[:]),
         ]
         for b, u, partial, last in closing:
             result = keep.tile([P, W], F32, name="result%d_%d" % (b, u))
-            nc.vector.tensor_tensor(result[:], partial, last[:], ADD)
+            nc.vector.tensor_tensor(result[:], partial, last, ADD)
             nc.sync.dma_start(out[b * P : (b + 1) * P, u * W : (u + 1) * W], result[:])

@@ -183,41 +183,16 @@ def tile_picked_gatedg_none_p_kernel(
                 nc.tensor.transpose(back[:, cols], turned[:, cols], ident[:])
             return back
 
-        def write_gate(b, d, src, func):
-            if (b, d) != (1, D - 1):
-                name = "gate%d_%d" % (b, d)
-                gates[b, d] = keep.tile([P, V], F32, name=name, tag=name)
-                nc.scalar.activation(gates[b, d][:], src[:], func)
-            else:
-                for u in range(2):
-                    name = "gate%d_%d_%d" % (b, d, u)
-                    gates[b, d, u] = keep.tile([P, W], F32, name=name, tag=name)
-                    nc.scalar.activation(gates[b, d, u][:], src[:, u * W : (u + 1) * W], func)
-
-        def gate(b, d, pieces=1):
+        def gate(b, d):
             pre = keep.tile([P, V], F32, name="pre%d_%d" % (b, d))
-            width = V // pieces
-            for n in range(pieces):
-                cols = slice(n * width, (n + 1) * width)
-                nc.vector.tensor_tensor(
-                    pre[:, cols],
-                    rows[1, b][:].indirect(pos_sb[d][:, n * width // 16 : (n + 1) * width // 16]),
-                    centres[b][:, cols],
-                    ADD,
-                )
-            write_gate(b, d, pre, SIGMOID)
+            nc.vector.tensor_tensor(pre[:], rows[1, b][:].indirect(pos_sb[d][:]), centres[b][:], ADD)
+            name = "gate%d_%d" % (b, d)
+            gates[b, d] = keep.tile([P, V], F32, name=name, tag=name)
+            nc.scalar.activation(gates[b, d][:], pre[:], SIGMOID)
 
-        def term(b, d, tag=None):
-            name = "term%d_%d" % (b, d)
-            tile = keep.tile([P, V], F32, name=name, tag=tag or name)
+        def term(b, d):
+            tile = keep.tile([P, V], F32, name="term%d_%d" % (b, d))
             nc.vector.tensor_tensor(tile[:], rows[2, b][:].indirect(pos_sb[d][:]), gates[b, d][:], MULT)
-            return tile
-
-        def last_term(b, u, tag):
-            tile = keep.tile([P, W], F32, name="last%d_%d" % (b, u), tag=tag)
-            nc.vector.tensor_tensor(
-                tile[:], rows[2, b][:].indirect(pos_sb[D - 1][:, u * W // 16 : (u + 1) * W // 16]), gates[b, D - 1, u][:], MULT
-            )
             return tile
 
         quantise([(1, 1), (2, 1)], "raw2_0")
@@ -230,32 +205,42 @@ def tile_picked_gatedg_none_p_kernel(
                 product(i, 1, hf * HALF, HALF)
 
         sum0 = sum_psum.tile([P, V], F32, name="sum0")
-        for d in range(D - 1):
-            add_turned(sum0[:], term(0, d)[:], d == 0, d == D - 2)
         for d in range(D):
-            gate(1, d)
-        partial0 = turn_back(leave(sum0[:], "turned0", COPY)[:])
+            add_turned(sum0[:], term(0, d)[:], d == 0, d == D - 1)
+        gate(1, 0)
+        back = turn_back(leave(sum0[:], "turned0", COPY)[:])
+        gate(1, 1)
+        result = keep.tile([P, V], F32, name="result0")
+        nc.scalar.copy(result[:], back[:])
+        nc.sync.dma_start(out[0:P, :], result[:])
+        gate(1, 2)
 
         sum1 = [sum_psum.tile([P, W], F32, name="sum1_%d" % u) for u in range(2)]
         for d in range(D - 1):
             tile = term(1, d)
-            for u in (1, 0):
-                add_turned(sum1[u][:], tile[:, u * W : (u + 1) * W], d == 0, u == 1 and d == D - 2)
-        partial1 = turn_back(leave(sum1[1][:], "turned1_1", COPY)[:])
-        add_turned(sum1[0][:], last_term(1, 0, "last1_0")[:], False, True)
-        back = turn_back(leave(sum1[0][:], "turned1_0", COPY)[:])
-        result = keep.tile([P, W], F32, name="result1_0")
-        nc.scalar.copy(result[:], back[:, 0:W])
-        nc.sync.dma_start(out[P : 2 * P, 0:W], result[:])
+            for u in range(2):
+                add_turned(sum1[u][:], tile[:, u * W : (u + 1) * W], d == 0, d == D - 2)
 
-        last0 = term(0, D - 1, "gate1_1")
-        last1 = last_term(1, 1, "last1_1")
-        closing = [
-            (0, 0, partial0[:, 0:W], last0[:, 0:W]),
-            (0, 1, partial0[:, W:V], last0[:, W:V]),
-            (1, 1, partial1[:, 0:W], last1[:]),
-        ]
-        for b, u, partial, last in closing:
-            result = keep.tile([P, W], F32, name="result%d_%d" % (b, u))
-            nc.vector.tensor_tensor(result[:], partial, last, ADD)
-            nc.sync.dma_start(out[b * P : (b + 1) * P, u * W : (u + 1) * W], result[:])
+        partial = []
+        last_gates = []
+        for u in range(2):
+            cols = slice(u * W, (u + 1) * W)
+            pre = keep.tile([P, W], F32, name="pre_last%d" % u, tag=("gate1_1", "term1_1")[u])
+            nc.vector.tensor_tensor(
+                pre[:], rows[1, 1][:].indirect(pos_sb[D - 1][:, u * W // 16 : (u + 1) * W // 16]), centres[1][:, cols], ADD
+            )
+            half_gate = keep.tile([P, W], F32, name="last_gate%d" % u)
+            nc.scalar.activation(half_gate[:], pre[:], SIGMOID)
+            last_gates.append(half_gate)
+            partial.append(turn_back(leave(sum1[u][:], "turned1_%d" % u, COPY)[:]))
+        lasts = []
+        for u in range(2):
+            tile = keep.tile([P, W], F32, name="last%d" % u)
+            nc.vector.tensor_tensor(
+                tile[:], rows[2, 1][:].indirect(pos_sb[D - 1][:, u * W // 16 : (u + 1) * W // 16]), last_gates[u][:], MULT
+            )
+            lasts.append(tile)
+        for u in range(2):
+            result = keep.tile([P, W], F32, name="result1_%d" % u)
+            nc.vector.tensor_tensor(result[:], partial[u][:, 0:W], lasts[u][:], ADD)
+            nc.sync.dma_start(out[P : 2 * P, u * W : (u + 1) * W], result[:])

@@ -51,22 +51,16 @@ def tile_picked_gatedg_none_p_kernel(
         words_sb = keep.tile([P, T], U16, name="words_sb")
         nc.sync.dma_start(words_sb[:].bitcast(I32), x_words[0].bitcast(I32))
 
-        raw = {}
+        def load_columns(name, src):
+            tile = keep.tile([P, PACK, src.shape[1]], F32, name=name, tag=name, align_bytes=64)
+            nc.sync.dma_start(tile[:], src.rearrange("(p j) c -> p j c", j=PACK))
+            return tile
 
-        def load_block(i, w, b):
-            name = "raw%d_%d" % (i, b)
-            tile = keep.tile([P, PACK, P], F32, name=name, tag=name, align_bytes=64)
-            nc.sync.dma_start(tile[:], w[:, b * P : (b + 1) * P].rearrange("(p j) c -> p j c", j=PACK))
-            raw[i, b] = tile[:]
-
-        load_block(0, w1, 0)
-        load_block(0, w1, 1)
-        load_block(1, w2, 0)
-        load_block(2, w3, 0)
+        raw1 = [load_columns("raw0_%d" % b, w1[:, b * P : (b + 1) * P]) for b in range(BLOCKS)]
+        raw2 = load_columns("raw1", w2)
+        raw3 = load_columns("raw2", w3)
         cen_sb = load_list("cen_sb", cen)
         pos_sb = [load_list("pos_sb%d" % d, p) for d, p in enumerate((pos1, pos2, pos3, pos4))]
-        load_block(1, w2, 1)
-        load_block(2, w3, 1)
 
         ident = keep.tile([P, P], F32, name="ident")
         make_identity(nc, ident[:])
@@ -89,20 +83,21 @@ def tile_picked_gatedg_none_p_kernel(
         codes = {}
         planes = {}
 
-        def quantise(parts, tag):
-            name = "%d_%d" % parts[0]
-            width = len(parts) * P
-            grouped = keep.tile([P, width, PACK], BF16, name="grouped" + name, tag=tag, align_bytes=64)
-            words = keep.tile([P, width], U32, name="codes" + name, tag="codes" + name, align_bytes=64)
-            plane = keep.tile([P, width], U8, name="planes" + name, align_bytes=64)
-            for n, part in enumerate(parts):
-                cols = slice(n * P, (n + 1) * P)
-                nc.scalar.copy(
-                    grouped[:, cols, :].rearrange("p (c i) t -> p c t i", i=4),
-                    raw[part].rearrange("p t (c i) -> p c t i", i=4),
+        def quantise(i, pieces):
+            grouped = keep.tile([P, N, PACK], BF16, name="grouped%d" % i, align_bytes=64)
+            words = keep.tile([P, N], U32, name="codes%d" % i, align_bytes=64)
+            plane = keep.tile([P, N], U8, name="planes%d" % i, align_bytes=64)
+            first = 0
+            for src, copy in pieces:
+                width = src.shape[2]
+                copy(
+                    grouped[:, first : first + width, :].rearrange("p (c i) t -> p c t i", i=4),
+                    src.rearrange("p t (c i) -> p c t i", i=4),
                 )
-                codes[part] = words[:, cols]
-                planes[part] = plane[:, cols]
+                first = first + width
+            for b in range(BLOCKS):
+                codes[i, b] = words[:, b * P : (b + 1) * P]
+                planes[i, b] = plane[:, b * P : (b + 1) * P]
             nc.vector.quantize_mx(
                 out=words[:].bitcast(FP8X4), scales=plane[:], in_=grouped[:].rearrange("p c t -> p (c t)")
             )
@@ -126,7 +121,7 @@ def tile_picked_gatedg_none_p_kernel(
 
         def empty(acc, i, b, first, width):
             if (i, b) not in rows:
-                rows[i, b] = keep.tile([P, S], F32, name="rows%d_%d" % (i, b), tag="raw2_0" if (i, b) == (0, 0) else "rows%d_%d" % (i, b), align_bytes=64)
+                rows[i, b] = keep.tile([P, S], F32, name="rows%d_%d" % (i, b), tag={(0, 0): "raw1", (0, 1): "raw2"}.get((i, b), "rows%d_%d" % (i, b)), align_bytes=64)
             nc.scalar.copy(rows[i, b][:, first : first + width], acc[:, 0:width])
 
         def product(i, b, first, width):
@@ -135,9 +130,10 @@ def tile_picked_gatedg_none_p_kernel(
         pick_words(0, 1, "picked_words0")
         picked_scales = keep.tile([P, S], U8, name="picked_scales", align_bytes=64)
         nc.vector.tensor_copy(picked_scales[:], scales_sb[:].indirect(offs_sb[:]))
-        quantise([(0, 0), (0, 1)], "grouped0_0")
+        quantise(0, [(tile[:], nc.scalar.copy) for tile in raw1])
         pick_words(1, 2, "raw0_1")
-        quantise([(1, 0), (2, 0)], "grouped1_0")
+        quantise(1, [(raw2[:], nc.scalar.copy)])
+        quantise(2, [(raw3[:, :, 0:P], nc.scalar.copy), (raw3[:, :, P:N], nc.vector.tensor_copy)])
         product(0, 0, 0, HALF)
         product(0, 0, HALF, HALF // 2)
         product(0, 0, HALF + HALF // 2, HALF // 2)
@@ -195,7 +191,6 @@ def tile_picked_gatedg_none_p_kernel(
             nc.vector.tensor_tensor(tile[:], rows[2, b][:].indirect(pos_sb[d][:]), gates[b, d][:], MULT)
             return tile
 
-        quantise([(1, 1), (2, 1)], "raw2_0")
         for hf in range(2):
             product(2, 0, hf * HALF, HALF)
         for d in range(D):

@@ -133,7 +133,7 @@ def tile_picked_gatedg_none_p_kernel(
         quantise(0, [(tile[:], nc.scalar.copy) for tile in raw1])
         pick_words(1, 2, "raw0_1")
         quantise(1, [(raw2[:], nc.scalar.copy)])
-        quantise(2, [(raw3[:, :, 0:P], nc.scalar.copy), (raw3[:, :, P:N], nc.vector.tensor_copy)])
+        quantise(2, [(raw3[:], nc.vector.tensor_copy)])
         product(0, 0, 0, HALF)
         product(0, 0, HALF, HALF // 2)
         product(0, 0, HALF + HALF // 2, HALF // 2)

@@ -64,8 +64,6 @@ def tile_picked_gatedg_none_p_kernel(
 
         ident = keep.tile([P, P], F32, name="ident")
         make_identity(nc, ident[:])
-        warm = keep.tile([P, 1], F32, name="warm")
-        nc.scalar.activation(warm[:], ident[:, 0:1], SIGMOID)
 
         picked_words = {}
 

@@ -40,6 +40,8 @@ def tile_picked_gatedg_none_p_kernel(
             nc.sync.dma_start(tile[:], src)
             return tile
 
+        words_sb = keep.tile([P, T], U16, name="words_sb", align_bytes=64)
+        nc.sync.dma_start(words_sb[:].bitcast(I32), x_words[0].bitcast(I32))
         offs_sb = load_list("offs_sb", offs)
 
         scales_sb = keep.tile([P, T], U8, name="scales_sb")
@@ -48,15 +50,13 @@ def tile_picked_gatedg_none_p_kernel(
             nc.sync.dma_start(
                 scales_sb[32 * q : 32 * q + 4, :].bitcast(I32), x_scales[0, 4 * q : 4 * q + 4, :].bitcast(I32)
             )
-        words_sb = keep.tile([P, T], U16, name="words_sb")
-        nc.sync.dma_start(words_sb[:].bitcast(I32), x_words[0].bitcast(I32))
 
         def load_columns(name, src):
             tile = keep.tile([P, PACK, src.shape[1]], F32, name=name, tag=name, align_bytes=64)
             nc.sync.dma_start(tile[:], src.rearrange("(p j) c -> p j c", j=PACK))
             return tile
 
-        raw1 = [load_columns("raw0_%d" % b, w1[:, b * P : (b + 1) * P]) for b in range(BLOCKS)]
+        raw1 = load_columns("raw0", w1)
         raw2 = load_columns("raw1", w2)
         raw3 = load_columns("raw2", w3)
         cen_sb = load_list("cen_sb", cen)
@@ -82,7 +82,7 @@ def tile_picked_gatedg_none_p_kernel(
         planes = {}
 
         def quantise(i, pieces):
-            grouped = keep.tile([P, N, PACK], BF16, name="grouped%d" % i, align_bytes=64)
+            grouped = keep.tile([P, N, PACK], BF16, name="grouped%d" % i, tag="words_sb" if i == 2 else "grouped%d" % i, align_bytes=64)
             words = keep.tile([P, N], U32, name="codes%d" % i, align_bytes=64)
             plane = keep.tile([P, N], U8, name="planes%d" % i, align_bytes=64)
             first = 0
@@ -128,8 +128,8 @@ def tile_picked_gatedg_none_p_kernel(
         pick_words(0, 1, "picked_words0")
         picked_scales = keep.tile([P, S], U8, name="picked_scales", align_bytes=64)
         nc.vector.tensor_copy(picked_scales[:], scales_sb[:].indirect(offs_sb[:]))
-        quantise(0, [(tile[:], nc.scalar.copy) for tile in raw1])
-        pick_words(1, 2, "raw0_1")
+        quantise(0, [(raw1[:], nc.scalar.copy)])
+        pick_words(1, 2, "raw0")
         quantise(1, [(raw2[:], nc.scalar.copy)])
         quantise(2, [(raw3[:], nc.vector.tensor_copy)])
         product(0, 0, 0, HALF)

@@ -24,6 +24,7 @@ PACK = 4
 HALF = 512
 BLOCKS = N // P
 D = 4
+ROWS = 16
 
 
 def tile_picked_gatedg_none_p_kernel(
@@ -32,6 +33,7 @@ def tile_picked_gatedg_none_p_kernel(
     nc = tc.nc
     with ExitStack() as ctx:
         keep = ctx.enter_context(tc.tile_pool(name="keep", bufs=1))
+        shared = ctx.enter_context(tc.tile_pool(name="shared", bufs=1))
         mm_psum = ctx.enter_context(tc.psum_pool(name="mm_psum", bufs=5))
         sum_psum = ctx.enter_context(tc.psum_pool(name="sum_psum", bufs=1))
 
@@ -40,27 +42,22 @@ def tile_picked_gatedg_none_p_kernel(
             nc.sync.dma_start(tile[:], src)
             return tile
 
-        words_sb = keep.tile([P, T], U16, name="words_sb", align_bytes=64)
-        nc.sync.dma_start(words_sb[:].bitcast(I32), x_words[0].bitcast(I32))
         offs_sb = load_list("offs_sb", offs)
 
         scales_sb = keep.tile([P, T], U8, name="scales_sb")
-        nc.gpsimd.memset(scales_sb[:].bitcast(I32), 0)
-        for q in range(4):
-            nc.sync.dma_start(
-                scales_sb[32 * q : 32 * q + 4, :].bitcast(I32), x_scales[0, 4 * q : 4 * q + 4, :].bitcast(I32)
-            )
+        nc.sync.dma_start(scales_sb[P - ROWS : P, :].bitcast(I32), x_scales[0].bitcast(I32))
+        nc.vector.memset(scales_sb[0 : P - ROWS, :].bitcast(I32), 0)
 
-        def load_columns(name, src):
-            tile = keep.tile([P, PACK, src.shape[1]], F32, name=name, tag=name, align_bytes=64)
+        def load_columns(pool, name, src, **place):
+            tile = pool.tile([P, PACK, N], F32, name=name, **place)
             nc.sync.dma_start(tile[:], src.rearrange("(p j) c -> p j c", j=PACK))
             return tile
 
-        raw1 = load_columns("raw0", w1)
-        raw2 = load_columns("raw1", w2)
-        raw3 = load_columns("raw2", w3)
-        cen_sb = load_list("cen_sb", cen)
-        pos_sb = [load_list("pos_sb%d" % d, p) for d, p in enumerate((pos1, pos2, pos3, pos4))]
+        raw1 = load_columns(keep, "raw0", w1, align_bytes=64)
+        words_sb = keep.tile([P, T], U16, name="words_sb", align_bytes=64)
+        nc.sync.dma_start(words_sb[:].bitcast(I32), x_words[0].bitcast(I32))
+        raw2 = load_columns(keep, "raw1", w2, align_bytes=64)
+        raw3 = load_columns(shared, "raw2", w3, offset=2048, align_bytes=64)
 
         ident = keep.tile([P, P], F32, name="ident")
         make_identity(nc, ident[:])
@@ -83,7 +80,10 @@ def tile_picked_gatedg_none_p_kernel(
 
         def quantise(i, pieces):
             grouped = keep.tile([P, N, PACK], BF16, name="grouped%d" % i, tag="words_sb" if i == 2 else "grouped%d" % i, align_bytes=64)
-            words = keep.tile([P, N], U32, name="codes%d" % i, align_bytes=64)
+            if i == 1:
+                words = shared.tile([P, N], U32, name="codes1", offset=4096, align_bytes=64)
+            else:
+                words = keep.tile([P, N], U32, name="codes%d" % i, align_bytes=64)
             plane = keep.tile([P, N], U8, name="planes%d" % i, align_bytes=64)
             first = 0
             for src, copy in pieces:
@@ -117,23 +117,34 @@ def tile_picked_gatedg_none_p_kernel(
             )
             return acc
 
-        def empty(acc, i, b, first, width):
+        def empty(acc, i, b, first, width, copy):
             if (i, b) not in rows:
-                rows[i, b] = keep.tile([P, S], F32, name="rows%d_%d" % (i, b), tag={(0, 0): "raw1", (0, 1): "raw2"}.get((i, b), "rows%d_%d" % (i, b)), align_bytes=64)
-            nc.scalar.copy(rows[i, b][:, first : first + width], acc[:, 0:width])
+                if i == 0:
+                    rows[i, b] = shared.tile([P, S], F32, name="rows0_%d" % b, offset=5120 * b, align_bytes=64)
+                else:
+                    rows[i, b] = keep.tile([P, S], F32, name="rows%d_%d" % (i, b), align_bytes=64)
+            copy(rows[i, b][:, first : first + width], acc[:, 0:width])
 
-        def product(i, b, first, width):
-            empty(multiply(i, b, first, width), i, b, first, width)
+        def product(i, b, first, width, copy=nc.scalar.copy):
+            empty(multiply(i, b, first, width), i, b, first, width, copy)
 
-        pick_words(0, 1, "picked_words0")
+        gathered_scales = keep.tile([P, S], U8, name="gathered_scales", align_bytes=64)
+        nc.vector.tensor_copy(gathered_scales[:], scales_sb[:].indirect(offs_sb[:]))
         picked_scales = keep.tile([P, S], U8, name="picked_scales", align_bytes=64)
-        nc.vector.tensor_copy(picked_scales[:], scales_sb[:].indirect(offs_sb[:]))
+        nc.gpsimd.memset(picked_scales[:].bitcast(I32), 0)
+        for r in range(4):
+            nc.sync.dma_start(
+                picked_scales[r:P:32, :].bitcast(I32), gathered_scales[P - ROWS + r : P : 4, :].bitcast(I32)
+            )
+        cen_sb = load_list("cen_sb", cen)
+        pos_sb = [load_list("pos_sb%d" % d, p) for d, p in enumerate((pos1, pos2, pos3, pos4))]
         quantise(0, [(raw1[:], nc.scalar.copy)])
-        pick_words(1, 2, "raw0")
+        pick_words(0, 1, "picked_words0")
+        pick_words(1, 1, "raw0")
         quantise(1, [(raw2[:], nc.scalar.copy)])
         quantise(2, [(raw3[:], nc.vector.tensor_copy)])
         product(0, 0, 0, HALF)
-        product(0, 0, HALF, HALF // 2)
+        product(0, 0, HALF, HALF // 2, nc.vector.tensor_copy)
         product(0, 0, HALF + HALF // 2, HALF // 2)
         for i, b in ((0, 1), (1, 0)):
             for hf in range(2):

@@ -33,7 +33,6 @@ def tile_picked_gatedg_none_p_kernel(
     nc = tc.nc
     with ExitStack() as ctx:
         keep = ctx.enter_context(tc.tile_pool(name="keep", bufs=1))
-        shared = ctx.enter_context(tc.tile_pool(name="shared", bufs=1))
         mm_psum = ctx.enter_context(tc.psum_pool(name="mm_psum", bufs=5))
         sum_psum = ctx.enter_context(tc.psum_pool(name="sum_psum", bufs=1))
 
@@ -45,7 +44,7 @@ def tile_picked_gatedg_none_p_kernel(
         offs_sb = load_list("offs_sb", offs)
 
         scales_sb = keep.tile([P, T], U8, name="scales_sb")
-        nc.sync.dma_start(scales_sb[P - ROWS : P, :].bitcast(I32), x_scales[0].bitcast(I32))
+        nc.scalar.dma_start(scales_sb[P - ROWS : P, :].bitcast(I32), x_scales[0].bitcast(I32))
         nc.vector.memset(scales_sb[0 : P - ROWS, :].bitcast(I32), 0)
 
         def load_columns(pool, name, src, **place):
@@ -56,8 +55,11 @@ def tile_picked_gatedg_none_p_kernel(
         raw1 = load_columns(keep, "raw0", w1, align_bytes=64)
         words_sb = keep.tile([P, T], U16, name="words_sb", align_bytes=64)
         nc.sync.dma_start(words_sb[:].bitcast(I32), x_words[0].bitcast(I32))
+        cen_sb = load_list("cen_sb", cen)
+        pos_sb = [load_list("pos_sb%d" % d, p) for d, p in enumerate((pos1, pos2))]
         raw2 = load_columns(keep, "raw1", w2, align_bytes=64)
-        raw3 = load_columns(shared, "raw2", w3, offset=2048, align_bytes=64)
+        raw3 = load_columns(keep, "raw2", w3, align_bytes=64)
+        pos_sb.extend(load_list("pos_sb%d" % (d + 2), p) for d, p in enumerate((pos3, pos4)))
 
         ident = keep.tile([P, P], F32, name="ident")
         make_identity(nc, ident[:])
@@ -80,10 +82,7 @@ def tile_picked_gatedg_none_p_kernel(
 
         def quantise(i, pieces):
             grouped = keep.tile([P, N, PACK], BF16, name="grouped%d" % i, tag="words_sb" if i == 2 else "grouped%d" % i, align_bytes=64)
-            if i == 1:
-                words = shared.tile([P, N], U32, name="codes1", offset=4096, align_bytes=64)
-            else:
-                words = keep.tile([P, N], U32, name="codes%d" % i, align_bytes=64)
+            words = keep.tile([P, N], U32, name="codes%d" % i, align_bytes=64)
             plane = keep.tile([P, N], U8, name="planes%d" % i, align_bytes=64)
             first = 0
             for src, copy in pieces:
@@ -119,10 +118,7 @@ def tile_picked_gatedg_none_p_kernel(
 
         def empty(acc, i, b, first, width, copy):
             if (i, b) not in rows:
-                if i == 0:
-                    rows[i, b] = shared.tile([P, S], F32, name="rows0_%d" % b, offset=5120 * b, align_bytes=64)
-                else:
-                    rows[i, b] = keep.tile([P, S], F32, name="rows%d_%d" % (i, b), align_bytes=64)
+                rows[i, b] = keep.tile([P, S], F32, name="rows%d_%d" % (i, b), align_bytes=64)
             copy(rows[i, b][:, first : first + width], acc[:, 0:width])
 
         def product(i, b, first, width, copy=nc.scalar.copy):
@@ -136,8 +132,6 @@ def tile_picked_gatedg_none_p_kernel(
             nc.sync.dma_start(
                 picked_scales[r:P:32, :].bitcast(I32), gathered_scales[P - ROWS + r : P : 4, :].bitcast(I32)
             )
-        cen_sb = load_list("cen_sb", cen)
-        pos_sb = [load_list("pos_sb%d" % d, p) for d, p in enumerate((pos1, pos2, pos3, pos4))]
         quantise(0, [(raw1[:], nc.scalar.copy)])
         pick_words(0, 1, "picked_words0")
         pick_words(1, 1, "raw0")

@@ -20,11 +20,17 @@ COPY = mybir.ActivationFunctionType.Copy
 SIGMOID = mybir.ActivationFunctionType.Sigmoid
 
 P = 128
+QUADRANT = 32
 PACK = 4
-HALF = 512
+SCALE_ROWS = K // 32
+ROWS_PER_QUADRANT = SCALE_ROWS * QUADRANT // P
+BANK = 512
+QUARTER = S // 4
 BLOCKS = N // P
 D = 4
-ROWS = 16
+W = V // 2
+PRODUCT_BANKS = 5
+Y, E, H = 0, 1, 2
 
 
 def tile_picked_gatedg_none_p_kernel(
@@ -33,7 +39,7 @@ def tile_picked_gatedg_none_p_kernel(
     nc = tc.nc
     with ExitStack() as ctx:
         keep = ctx.enter_context(tc.tile_pool(name="keep", bufs=1))
-        mm_psum = ctx.enter_context(tc.psum_pool(name="mm_psum", bufs=5))
+        mm_psum = ctx.enter_context(tc.psum_pool(name="mm_psum", bufs=PRODUCT_BANKS))
         sum_psum = ctx.enter_context(tc.psum_pool(name="sum_psum", bufs=1))
 
         def load_list(name, src):
@@ -41,176 +47,152 @@ def tile_picked_gatedg_none_p_kernel(
             nc.sync.dma_start(tile[:], src)
             return tile
 
-        offs_sb = load_list("offs_sb", offs)
+        def entries(list_tile, first, count):
+            return list_tile[:, first // 16 : (first + count) // 16]
 
-        scales_sb = keep.tile([P, T], U8, name="scales_sb")
-        nc.scalar.dma_start(scales_sb[P - ROWS : P, :].bitcast(I32), x_scales[0].bitcast(I32))
-        nc.vector.memset(scales_sb[0 : P - ROWS, :].bitcast(I32), 0)
-
-        def load_columns(pool, name, src, **place):
-            tile = pool.tile([P, PACK, N], F32, name=name, **place)
+        def load_weight(name, src):
+            tile = keep.tile([P, PACK, N], F32, name=name, align_bytes=64)
             nc.sync.dma_start(tile[:], src.rearrange("(p j) c -> p j c", j=PACK))
             return tile
 
-        raw1 = load_columns(keep, "raw0", w1, align_bytes=64)
+        offs_sb = load_list("offs_sb", offs)
+        scales_sb = keep.tile([P, T], U8, name="scales_sb")
+        nc.scalar.dma_start(scales_sb[P - SCALE_ROWS : P, :].bitcast(I32), x_scales[0].bitcast(I32))
+        nc.vector.memset(scales_sb[0 : P - SCALE_ROWS, :].bitcast(I32), 0)
+
+        raw_y = load_weight("raw_y", w1)
         words_sb = keep.tile([P, T], U16, name="words_sb", align_bytes=64)
         nc.sync.dma_start(words_sb[:].bitcast(I32), x_words[0].bitcast(I32))
         cen_sb = load_list("cen_sb", cen)
-        pos_sb = [load_list("pos_sb%d" % d, p) for d, p in enumerate((pos1, pos2))]
-        raw2 = load_columns(keep, "raw1", w2, align_bytes=64)
-        raw3 = load_columns(keep, "raw2", w3, align_bytes=64)
-        pos_sb.extend(load_list("pos_sb%d" % (d + 2), p) for d, p in enumerate((pos3, pos4)))
+        raw_e = load_weight("raw_e", w2)
+        raw_h = load_weight("raw_h", w3)
+        pos_sb = [load_list("pos_sb0", pos1), load_list("pos_sb1", pos2)]
 
         ident = keep.tile([P, P], F32, name="ident")
         make_identity(nc, ident[:])
 
         picked_words = {}
 
-        def pick_words(hf, pieces, tag):
-            tile = keep.tile([P, HALF], U16, name="picked_words%d" % hf, tag=tag, align_bytes=64)
-            width = HALF // pieces
-            for n in range(pieces):
-                first = hf * HALF + n * width
-                nc.vector.tensor_copy(
-                    tile[:, n * width : (n + 1) * width],
-                    words_sb[:].indirect(offs_sb[:, first // 16 : (first + width) // 16]),
-                )
-            picked_words[hf] = tile
+        def pick_words(half, tag):
+            tile = keep.tile([P, BANK], U16, name="picked_words%d" % half, tag=tag, align_bytes=64)
+            nc.vector.tensor_copy(tile[:], words_sb[:].indirect(entries(offs_sb, half * BANK, BANK)))
+            picked_words[half] = tile
 
         codes = {}
-        planes = {}
+        weight_scales = {}
 
-        def quantise(i, pieces):
-            grouped = keep.tile([P, N, PACK], BF16, name="grouped%d" % i, tag="words_sb" if i == 2 else "grouped%d" % i, align_bytes=64)
-            words = keep.tile([P, N], U32, name="codes%d" % i, align_bytes=64)
-            plane = keep.tile([P, N], U8, name="planes%d" % i, align_bytes=64)
-            first = 0
-            for src, copy in pieces:
-                width = src.shape[2]
-                copy(
-                    grouped[:, first : first + width, :].rearrange("p (c i) t -> p c t i", i=4),
-                    src.rearrange("p t (c i) -> p c t i", i=4),
-                )
-                first = first + width
-            for b in range(BLOCKS):
-                codes[i, b] = words[:, b * P : (b + 1) * P]
-                planes[i, b] = plane[:, b * P : (b + 1) * P]
-            nc.vector.quantize_mx(
-                out=words[:].bitcast(FP8X4), scales=plane[:], in_=grouped[:].rearrange("p c t -> p (c t)")
+        def quantise(i, raw, copy, tag):
+            grouped = keep.tile([P, N, PACK], BF16, name="grouped%d" % i, tag=tag, align_bytes=64)
+            code_tile = keep.tile([P, N], U32, name="codes%d" % i, align_bytes=64)
+            scale_tile = keep.tile([P, N], U8, name="weight_scales%d" % i, align_bytes=64)
+            copy(
+                grouped[:].rearrange("p (c i) t -> p c t i", i=4),
+                raw[:].rearrange("p t (c i) -> p c t i", i=4),
             )
+            nc.vector.quantize_mx(
+                out=code_tile[:].bitcast(FP8X4), scales=scale_tile[:], in_=grouped[:].rearrange("p c t -> p (c t)")
+            )
+            for b in range(BLOCKS):
+                codes[i, b] = code_tile[:, b * P : (b + 1) * P]
+                weight_scales[i, b] = scale_tile[:, b * P : (b + 1) * P]
+
+        gathered_scales = keep.tile([P, S], U8, name="gathered_scales", align_bytes=64)
+        nc.vector.tensor_copy(gathered_scales[:], scales_sb[:].indirect(offs_sb[:]))
+        node_scales = keep.tile([P, S], U8, name="node_scales", align_bytes=64)
+        nc.gpsimd.memset(node_scales[:].bitcast(I32), 0)
+        for r in range(ROWS_PER_QUADRANT):
+            nc.sync.dma_start(
+                node_scales[r:P:QUADRANT, :].bitcast(I32),
+                gathered_scales[P - SCALE_ROWS + r : P : ROWS_PER_QUADRANT, :].bitcast(I32),
+            )
+        pos_sb.extend([load_list("pos_sb2", pos3), load_list("pos_sb3", pos4)])
+
+        quantise(Y, raw_y, nc.scalar.copy, "grouped_y")
+        pick_words(0, "picked_words0")
+        pick_words(1, "raw_y")
+        quantise(E, raw_e, nc.scalar.copy, "grouped_e")
+        quantise(H, raw_h, nc.vector.tensor_copy, "words_sb")
 
         rows = {}
 
-        def multiply(i, b, first, width):
-            acc = mm_psum.tile([P, HALF], F32, name="acc")
-            cols = slice(first, first + width)
-            hf, start = divmod(first, HALF)
+        def product(i, b, first, width, copy=nc.scalar.copy):
+            acc = mm_psum.tile([P, BANK], F32, name="acc")
+            half, start = divmod(first, BANK)
             nc.tensor.matmul_mx(
                 out=acc[:, 0:width],
                 lhsT=codes[i, b].bitcast(FP8X4),
-                lhsT_scale=planes[i, b],
-                rhs=picked_words[hf][:, start : start + width].bitcast(FP4X4),
-                rhs_scale=picked_scales[:, cols],
+                lhsT_scale=weight_scales[i, b],
+                rhs=picked_words[half][:, start : start + width].bitcast(FP4X4),
+                rhs_scale=node_scales[:, first : first + width],
                 start=True,
                 stop=True,
             )
-            return acc
-
-        def empty(acc, i, b, first, width, copy):
             if (i, b) not in rows:
                 rows[i, b] = keep.tile([P, S], F32, name="rows%d_%d" % (i, b), align_bytes=64)
             copy(rows[i, b][:, first : first + width], acc[:, 0:width])
 
-        def product(i, b, first, width, copy=nc.scalar.copy):
-            empty(multiply(i, b, first, width), i, b, first, width, copy)
+        def whole_product(i, b):
+            for half in range(2):
+                product(i, b, half * BANK, BANK)
 
-        gathered_scales = keep.tile([P, S], U8, name="gathered_scales", align_bytes=64)
-        nc.vector.tensor_copy(gathered_scales[:], scales_sb[:].indirect(offs_sb[:]))
-        picked_scales = keep.tile([P, S], U8, name="picked_scales", align_bytes=64)
-        nc.gpsimd.memset(picked_scales[:].bitcast(I32), 0)
-        for r in range(4):
-            nc.sync.dma_start(
-                picked_scales[r:P:32, :].bitcast(I32), gathered_scales[P - ROWS + r : P : 4, :].bitcast(I32)
-            )
-        quantise(0, [(raw1[:], nc.scalar.copy)])
-        pick_words(0, 1, "picked_words0")
-        pick_words(1, 1, "raw0")
-        quantise(1, [(raw2[:], nc.scalar.copy)])
-        quantise(2, [(raw3[:], nc.vector.tensor_copy)])
-        product(0, 0, 0, HALF)
-        product(0, 0, HALF, HALF // 2, nc.vector.tensor_copy)
-        product(0, 0, HALF + HALF // 2, HALF // 2)
-        for i, b in ((0, 1), (1, 0)):
-            for hf in range(2):
-                product(i, b, hf * HALF, HALF)
+        quarter_copies = (nc.scalar.copy, nc.scalar.copy, nc.vector.tensor_copy, nc.scalar.copy)
+        for n, copy in enumerate(quarter_copies):
+            product(Y, 0, n * QUARTER, QUARTER, copy)
+        whole_product(Y, 1)
+        whole_product(E, 0)
 
-        centres = {}
+        centres = []
+        for b in range(BLOCKS):
+            centre = keep.tile([P, V], F32, name="centre%d" % b)
+            nc.vector.tensor_copy(centre[:], rows[Y, b][:].indirect(cen_sb[:]))
+            centres.append(centre)
 
-        def centre(b, pieces):
-            centres[b] = keep.tile([P, V], F32, name="centre%d" % b)
-            width = V // pieces
-            for n in range(pieces):
-                nc.vector.tensor_copy(
-                    centres[b][:, n * width : (n + 1) * width],
-                    rows[0, b][:].indirect(cen_sb[:, n * width // 16 : (n + 1) * width // 16]),
-                )
-
-        centre(0, 1)
-        centre(1, 1)
-
-        W = V // 2
         gates = {}
-
-        def add_turned(acc, src, first, last):
-            chunks = src.shape[1] // P
-            for c in range(chunks):
-                cols = slice(c * P, (c + 1) * P)
-                nc.tensor.matmul(
-                    acc[:, cols], src[:, cols], ident[:], is_transpose=True,
-                    start=(first and c == 0), stop=(last and c == chunks - 1),
-                )
-
-        def leave(acc, name, func):
-            turned = keep.tile([P, acc.shape[1]], F32, name=name)
-            nc.scalar.activation(turned[:], acc, func)
-            return turned
-
-        def turn_back(turned):
-            back = mm_psum.tile([P, HALF], F32, name="acc")
-            for c in range(turned.shape[1] // P):
-                cols = slice(c * P, (c + 1) * P)
-                nc.tensor.transpose(back[:, cols], turned[:, cols], ident[:])
-            return back
 
         def gate(b, d):
             pre = keep.tile([P, V], F32, name="pre%d_%d" % (b, d))
-            nc.vector.tensor_tensor(pre[:], rows[1, b][:].indirect(pos_sb[d][:]), centres[b][:], ADD)
-            name = "gate%d_%d" % (b, d)
-            gates[b, d] = keep.tile([P, V], F32, name=name, tag=name)
+            nc.vector.tensor_tensor(pre[:], rows[E, b][:].indirect(pos_sb[d][:]), centres[b][:], ADD)
+            gates[b, d] = keep.tile([P, V], F32, name="gate%d_%d" % (b, d))
             nc.scalar.activation(gates[b, d][:], pre[:], SIGMOID)
 
         def term(b, d):
             tile = keep.tile([P, V], F32, name="term%d_%d" % (b, d))
-            nc.vector.tensor_tensor(tile[:], rows[2, b][:].indirect(pos_sb[d][:]), gates[b, d][:], MULT)
+            nc.vector.tensor_tensor(tile[:], rows[H, b][:].indirect(pos_sb[d][:]), gates[b, d][:], MULT)
             return tile
 
-        for hf in range(2):
-            product(2, 0, hf * HALF, HALF)
+        def add_turned(total, src, opens, closes):
+            chunks = src.shape[1] // P
+            for c in range(chunks):
+                cols = slice(c * P, (c + 1) * P)
+                nc.tensor.matmul(
+                    total[:, cols], src[:, cols], ident[:], is_transpose=True,
+                    start=(opens and c == 0), stop=(closes and c == chunks - 1),
+                )
+
+        def turn_back(total, name):
+            turned = keep.tile([P, total.shape[1]], F32, name=name)
+            nc.scalar.activation(turned[:], total, COPY)
+            back = mm_psum.tile([P, BANK], F32, name="acc")
+            for c in range(total.shape[1] // P):
+                cols = slice(c * P, (c + 1) * P)
+                nc.tensor.transpose(back[:, cols], turned[:, cols], ident[:])
+            return back
+
+        whole_product(H, 0)
         for d in range(D):
             gate(0, d)
-        for i in (1, 2):
-            for hf in range(2):
-                product(i, 1, hf * HALF, HALF)
+        whole_product(E, 1)
+        whole_product(H, 1)
 
         sum0 = sum_psum.tile([P, V], F32, name="sum0")
         for d in range(D):
             add_turned(sum0[:], term(0, d)[:], d == 0, d == D - 1)
         gate(1, 0)
-        back = turn_back(leave(sum0[:], "turned0", COPY)[:])
+        back0 = turn_back(sum0[:], "turned0")
         gate(1, 1)
-        result = keep.tile([P, V], F32, name="result0")
-        nc.scalar.copy(result[:], back[:])
-        nc.sync.dma_start(out[0:P, :], result[:])
+        result0 = keep.tile([P, V], F32, name="result0")
+        nc.scalar.copy(result0[:], back0[:])
+        nc.sync.dma_start(out[0:P, :], result0[:])
         gate(1, 2)
 
         sum1 = [sum_psum.tile([P, W], F32, name="sum1_%d" % u) for u in range(2)]
@@ -219,26 +201,26 @@ def tile_picked_gatedg_none_p_kernel(
             for u in range(2):
                 add_turned(sum1[u][:], tile[:, u * W : (u + 1) * W], d == 0, d == D - 2)
 
+        last = D - 1
         partial = []
         last_gates = []
-        for u in range(2):
-            cols = slice(u * W, (u + 1) * W)
-            pre = keep.tile([P, W], F32, name="pre_last%d" % u, tag=("gate1_1", "term1_1")[u])
+        for u, tag in enumerate(("gate1_1", "term1_1")):
+            pre = keep.tile([P, W], F32, name="pre_last%d" % u, tag=tag)
             nc.vector.tensor_tensor(
-                pre[:], rows[1, 1][:].indirect(pos_sb[D - 1][:, u * W // 16 : (u + 1) * W // 16]), centres[1][:, cols], ADD
+                pre[:], rows[E, 1][:].indirect(entries(pos_sb[last], u * W, W)), centres[1][:, u * W : (u + 1) * W], ADD
             )
             half_gate = keep.tile([P, W], F32, name="last_gate%d" % u)
             nc.scalar.activation(half_gate[:], pre[:], SIGMOID)
             last_gates.append(half_gate)
-            partial.append(turn_back(leave(sum1[u][:], "turned1_%d" % u, COPY)[:]))
-        lasts = []
+            partial.append(turn_back(sum1[u][:], "turned1_%d" % u))
+        last_terms = []
         for u in range(2):
-            tile = keep.tile([P, W], F32, name="last%d" % u)
+            half_term = keep.tile([P, W], F32, name="last_term%d" % u)
             nc.vector.tensor_tensor(
-                tile[:], rows[2, 1][:].indirect(pos_sb[D - 1][:, u * W // 16 : (u + 1) * W // 16]), last_gates[u][:], MULT
+                half_term[:], rows[H, 1][:].indirect(entries(pos_sb[last], u * W, W)), last_gates[u][:], MULT
             )
-            lasts.append(tile)
+            last_terms.append(half_term)
         for u in range(2):
-            result = keep.tile([P, W], F32, name="result1_%d" % u)
-            nc.vector.tensor_tensor(result[:], partial[u][:, 0:W], lasts[u][:], ADD)
-            nc.sync.dma_start(out[P : 2 * P, u * W : (u + 1) * W], result[:])
+            result1 = keep.tile([P, W], F32, name="result1_%d" % u)
+            nc.vector.tensor_tensor(result1[:], partial[u][:, 0:W], last_terms[u][:], ADD)
+            nc.sync.dma_start(out[P : 2 * P, u * W : (u + 1) * W], result1[:])

@@ -63,10 +63,7 @@ def tile_picked_gatedg_none_p_kernel(
         raw_y = load_weight("raw_y", w1)
         words_sb = keep.tile([P, T], U16, name="words_sb", align_bytes=64)
         nc.sync.dma_start(words_sb[:].bitcast(I32), x_words[0].bitcast(I32))
-        cen_sb = load_list("cen_sb", cen)
         raw_e = load_weight("raw_e", w2)
-        raw_h = load_weight("raw_h", w3)
-        pos_sb = [load_list("pos_sb0", pos1), load_list("pos_sb1", pos2)]
 
         ident = keep.tile([P, P], F32, name="ident")
         make_identity(nc, ident[:])
@@ -105,13 +102,14 @@ def tile_picked_gatedg_none_p_kernel(
                 node_scales[r:P:QUADRANT, :].bitcast(I32),
                 gathered_scales[P - SCALE_ROWS + r : P : ROWS_PER_QUADRANT, :].bitcast(I32),
             )
-        pos_sb.extend([load_list("pos_sb2", pos3), load_list("pos_sb3", pos4)])
+        cen_sb = load_list("cen_sb", cen)
+        raw_h = load_weight("raw_h", w3)
+        pos_sb = [load_list("pos_sb%d" % n, src) for n, src in enumerate((pos1, pos2, pos3, pos4))]
 
         quantise(Y, raw_y, nc.scalar.copy, "grouped_y")
         pick_words(0, "picked_words0")
         pick_words(1, "raw_y")
         quantise(E, raw_e, nc.scalar.copy, "grouped_e")
-        quantise(H, raw_h, nc.vector.tensor_copy, "words_sb")
 
         rows = {}
 
@@ -149,11 +147,12 @@ def tile_picked_gatedg_none_p_kernel(
 
         gates = {}
 
-        def gate(b, d):
-            pre = keep.tile([P, V], F32, name="pre%d_%d" % (b, d))
-            nc.vector.tensor_tensor(pre[:], rows[E, b][:].indirect(pos_sb[d][:]), centres[b][:], ADD)
+        def gate(b, d, pre=None):
+            if pre is None:
+                pre = keep.tile([P, V], F32, name="pre%d_%d" % (b, d))[:]
+            nc.vector.tensor_tensor(pre, rows[E, b][:].indirect(pos_sb[d][:]), centres[b][:], ADD)
             gates[b, d] = keep.tile([P, V], F32, name="gate%d_%d" % (b, d))
-            nc.scalar.activation(gates[b, d][:], pre[:], SIGMOID)
+            nc.scalar.activation(gates[b, d][:], pre, SIGMOID)
 
         def term(b, d):
             tile = keep.tile([P, V], F32, name="term%d_%d" % (b, d))
@@ -178,9 +177,12 @@ def tile_picked_gatedg_none_p_kernel(
                 nc.tensor.transpose(back[:, cols], turned[:, cols], ident[:])
             return back
 
+        quantise(H, raw_h, nc.scalar.copy, "grouped_h")
         whole_product(H, 0)
-        for d in range(D):
-            gate(0, d)
+        gate(0, 0)
+        held = keep.tile([P, D - 1, V], F32, name="held", tag="raw_h", align_bytes=64)
+        for d in range(1, D):
+            gate(0, d, held[:, d - 1, :])
         whole_product(E, 1)
         whole_product(H, 1)
 

@@ -60,19 +60,30 @@ def tile_picked_gatedg_none_p_kernel(
         nc.scalar.dma_start(scales_sb[P - SCALE_ROWS : P, :].bitcast(I32), x_scales[0].bitcast(I32))
         nc.vector.memset(scales_sb[0 : P - SCALE_ROWS, :].bitcast(I32), 0)
 
-        raw_y = load_weight("raw_y", w1)
+        raw_y = keep.tile([P, PACK, N], F32, name="raw_y", align_bytes=64)
+        w1_rows = w1.rearrange("(p j) c -> p j c", j=PACK)
+        nc.sync.dma_start(raw_y[:, 0:2, :], w1_rows[:, 0:2, :])
+        nc.scalar.dma_start(raw_y[:, 2:4, :], w1_rows[:, 2:4, :])
         words_sb = keep.tile([P, T], U16, name="words_sb", align_bytes=64)
         nc.sync.dma_start(words_sb[:].bitcast(I32), x_words[0].bitcast(I32))
         raw_e = load_weight("raw_e", w2)
 
         ident = keep.tile([P, P], F32, name="ident")
         make_identity(nc, ident[:])
+        warm = keep.tile([P, 1], F32, name="warm")
+        zero = keep.tile([P, 1], F32, name="zero")
+        nc.vector.memset(zero[:], 0.0)
+        nc.scalar.activation(warm[:], zero[:], SIGMOID)
 
         picked_words = {}
 
-        def pick_words(half, tag):
+        def pick_words(half, tag, pieces=1):
             tile = keep.tile([P, BANK], U16, name="picked_words%d" % half, tag=tag, align_bytes=64)
-            nc.vector.tensor_copy(tile[:], words_sb[:].indirect(entries(offs_sb, half * BANK, BANK)))
+            width = BANK // pieces
+            for first in range(0, BANK, width):
+                nc.vector.tensor_copy(
+                    tile[:, first : first + width], words_sb[:].indirect(entries(offs_sb, half * BANK + first, width))
+                )
             picked_words[half] = tile
 
         codes = {}
@@ -95,10 +106,12 @@ def tile_picked_gatedg_none_p_kernel(
 
         gathered_scales = keep.tile([P, S], U8, name="gathered_scales", align_bytes=64)
         nc.vector.tensor_copy(gathered_scales[:], scales_sb[:].indirect(offs_sb[:]))
+        quantise(Y, raw_y, nc.scalar.copy, "grouped_y")
         node_scales = keep.tile([P, S], U8, name="node_scales", align_bytes=64)
         nc.gpsimd.memset(node_scales[:].bitcast(I32), 0)
         for r in range(ROWS_PER_QUADRANT):
-            nc.sync.dma_start(
+            queue = nc.sync if r < 2 else nc.scalar
+            queue.dma_start(
                 node_scales[r:P:QUADRANT, :].bitcast(I32),
                 gathered_scales[P - SCALE_ROWS + r : P : ROWS_PER_QUADRANT, :].bitcast(I32),
             )
@@ -106,9 +119,8 @@ def tile_picked_gatedg_none_p_kernel(
         raw_h = load_weight("raw_h", w3)
         pos_sb = [load_list("pos_sb%d" % n, src) for n, src in enumerate((pos1, pos2, pos3, pos4))]
 
-        quantise(Y, raw_y, nc.scalar.copy, "grouped_y")
         pick_words(0, "picked_words0")
-        pick_words(1, "raw_y")
+        pick_words(1, "raw_y", 2)
         quantise(E, raw_e, nc.scalar.copy, "grouped_e")
 
         rows = {}

@@ -121,7 +121,7 @@ def tile_picked_gatedg_none_p_kernel(
 
         pick_words(0, "picked_words0")
         pick_words(1, "raw_y", 2)
-        quantise(E, raw_e, nc.scalar.copy, "grouped_e")
+        quantise(E, raw_e, nc.vector.tensor_copy, "words_sb")
 
         rows = {}
 
@@ -145,7 +145,7 @@ def tile_picked_gatedg_none_p_kernel(
             for half in range(2):
                 product(i, b, half * BANK, BANK)
 
-        quarter_copies = (nc.scalar.copy, nc.scalar.copy, nc.vector.tensor_copy, nc.scalar.copy)
+        quarter_copies = (nc.scalar.copy, nc.scalar.copy, nc.scalar.copy, nc.scalar.copy)
         for n, copy in enumerate(quarter_copies):
             product(Y, 0, n * QUARTER, QUARTER, copy)
         whole_product(Y, 1)

@@ -66,7 +66,9 @@ def tile_picked_gatedg_none_p_kernel(
         nc.scalar.dma_start(raw_y[:, 2:4, :], w1_rows[:, 2:4, :])
         words_sb = keep.tile([P, T], U16, name="words_sb", align_bytes=64)
         nc.sync.dma_start(words_sb[:].bitcast(I32), x_words[0].bitcast(I32))
-        raw_e = load_weight("raw_e", w2)
+        raw_e = keep.tile([P, PACK, N], F32, name="raw_e", align_bytes=64)
+        w2_rows = w2.rearrange("(p j) c -> p j c", j=PACK)
+        nc.sync.dma_start(raw_e[:, 0:2, :], w2_rows[:, 0:2, :])
 
         ident = keep.tile([P, P], F32, name="ident")
         make_identity(nc, ident[:])
@@ -115,6 +117,7 @@ def tile_picked_gatedg_none_p_kernel(
                 node_scales[r:P:QUADRANT, :].bitcast(I32),
                 gathered_scales[P - SCALE_ROWS + r : P : ROWS_PER_QUADRANT, :].bitcast(I32),
             )
+        nc.sync.dma_start(raw_e[:, 2:4, :], w2_rows[:, 2:4, :])
         cen_sb = load_list("cen_sb", cen)
         raw_h = load_weight("raw_h", w3)
         pos_sb = [load_list("pos_sb%d" % n, src) for n, src in enumerate((pos1, pos2, pos3, pos4))]

@@ -29,7 +29,6 @@ QUARTER = S // 4
 BLOCKS = N // P
 D = 4
 W = V // 2
-PRODUCT_BANKS = 5
 Y, E, H = 0, 1, 2
 
 
@@ -39,8 +38,7 @@ def tile_picked_gatedg_none_p_kernel(
     nc = tc.nc
     with ExitStack() as ctx:
         keep = ctx.enter_context(tc.tile_pool(name="keep", bufs=1))
-        mm_psum = ctx.enter_context(tc.psum_pool(name="mm_psum", bufs=PRODUCT_BANKS))
-        sum_psum = ctx.enter_context(tc.psum_pool(name="sum_psum", bufs=1))
+        psum = ctx.enter_context(tc.psum_pool(name="psum", bufs=1))
 
         def load_list(name, src):
             tile = keep.tile(list(src.shape), U16, name=name)
@@ -128,8 +126,11 @@ def tile_picked_gatedg_none_p_kernel(
 
         rows = {}
 
-        def product(i, b, first, width, copy=nc.scalar.copy):
-            acc = mm_psum.tile([P, BANK], F32, name="acc")
+        def bank(number, name):
+            return psum.tile([P, BANK], F32, name=name, tag="bank%d" % number)
+
+        def product(i, b, first, width, number, copy=nc.scalar.copy):
+            acc = bank(number, "acc%d_%d_%d" % (i, b, first))
             half, start = divmod(first, BANK)
             nc.tensor.matmul_mx(
                 out=acc[:, 0:width],
@@ -144,34 +145,13 @@ def tile_picked_gatedg_none_p_kernel(
                 rows[i, b] = keep.tile([P, S], F32, name="rows%d_%d" % (i, b), align_bytes=64)
             copy(rows[i, b][:, first : first + width], acc[:, 0:width])
 
-        def whole_product(i, b):
+        def whole_product(i, b, number):
             for half in range(2):
-                product(i, b, half * BANK, BANK)
+                product(i, b, half * BANK, BANK, number + half)
 
-        quarter_copies = (nc.scalar.copy, nc.scalar.copy, nc.scalar.copy, nc.scalar.copy)
-        for n, copy in enumerate(quarter_copies):
-            product(Y, 0, n * QUARTER, QUARTER, copy)
-        whole_product(Y, 1)
-        whole_product(E, 0)
-
-        centres = []
-        for b in range(BLOCKS):
-            centre = keep.tile([P, V], F32, name="centre%d" % b)
-            nc.vector.tensor_copy(centre[:], rows[Y, b][:].indirect(cen_sb[:]))
-            centres.append(centre)
-
-        gates = {}
-
-        def gate(b, d, pre=None):
-            if pre is None:
-                pre = keep.tile([P, V], F32, name="pre%d_%d" % (b, d))[:]
-            nc.vector.tensor_tensor(pre, rows[E, b][:].indirect(pos_sb[d][:]), centres[b][:], ADD)
-            gates[b, d] = keep.tile([P, V], F32, name="gate%d_%d" % (b, d))
-            nc.scalar.activation(gates[b, d][:], pre, SIGMOID)
-
-        def term(b, d):
-            tile = keep.tile([P, V], F32, name="term%d_%d" % (b, d))
-            nc.vector.tensor_tensor(tile[:], rows[H, b][:].indirect(pos_sb[d][:]), gates[b, d][:], MULT)
+        def scalar_gather(name, window, list_tile):
+            tile = keep.tile([P, V], F32, name=name)
+            nc.scalar.activation(tile[:], window[:].indirect(list_tile[:]), COPY)
             return tile
 
         def add_turned(total, src, opens, closes):
@@ -183,58 +163,102 @@ def tile_picked_gatedg_none_p_kernel(
                     start=(opens and c == 0), stop=(closes and c == chunks - 1),
                 )
 
-        def turn_back(total, name):
-            turned = keep.tile([P, total.shape[1]], F32, name=name)
-            nc.scalar.activation(turned[:], total, COPY)
-            back = mm_psum.tile([P, BANK], F32, name="acc")
-            for c in range(total.shape[1] // P):
-                cols = slice(c * P, (c + 1) * P)
-                nc.tensor.transpose(back[:, cols], turned[:, cols], ident[:])
-            return back
+        centres = {}
+        sums = {}
+        gates = {}
 
-        quantise(H, raw_h, nc.scalar.copy, "grouped_h")
-        whole_product(H, 0)
-        gate(0, 0)
-        held = keep.tile([P, D - 1, V], F32, name="held", tag="raw_h", align_bytes=64)
-        for d in range(1, D):
-            gate(0, d, held[:, d - 1, :])
-        whole_product(E, 1)
-        whole_product(H, 1)
+        def gate_sum(b, d):
+            sums[b, d] = keep.tile([P, V], F32, name="pre%d_%d" % (b, d))
+            nc.vector.tensor_tensor(sums[b, d][:], rows[E, b][:].indirect(pos_sb[d][:]), centres[b][:], ADD)
 
-        sum0 = sum_psum.tile([P, V], F32, name="sum0")
+        def gate(b, d):
+            gates[b, d] = keep.tile([P, V], F32, name="gate%d_%d" % (b, d))
+            nc.scalar.activation(gates[b, d][:], sums[b, d][:], SIGMOID)
+
+        def term(b, d):
+            tile = keep.tile([P, V], F32, name="term%d_%d" % (b, d))
+            nc.vector.tensor_tensor(tile[:], rows[H, b][:].indirect(pos_sb[d][:]), gates[b, d][:], MULT)
+            return tile
+
+        def turned_gate_sum(b, d, number):
+            sums[b, d] = bank(number, "pre%d_%d" % (b, d))
+            add_turned(sums[b, d][:], centres[b][:], True, False)
+            add_turned(sums[b, d][:], scalar_gather("e_picked%d_%d" % (b, d), rows[E, b], pos_sb[d])[:], False, True)
+
+        def turned_message(b, d, number):
+            turned = bank(number, "message%d_%d" % (b, d))
+            add_turned(turned[:], scalar_gather("h_picked%d_%d" % (b, d), rows[H, b], pos_sb[d])[:], True, True)
+            return turned
+
+        def turned_term(b, d, message):
+            tile = keep.tile([P, V], F32, name="term%d_%d" % (b, d))
+            nc.vector.tensor_tensor(tile[:], message[:], gates[b, d][:], MULT)
+            return tile
+
+        def to_sbuf(total, name):
+            tile = keep.tile([P, total.shape[1]], F32, name=name)
+            nc.scalar.copy(tile[:], total)
+            return tile
+
+        for n in range(4):
+            product(Y, 0, n * QUARTER, QUARTER, n)
+        whole_product(E, 0, 4)
+        centres[0] = keep.tile([P, V], F32, name="centre0")
+        nc.vector.tensor_copy(centres[0][:], rows[Y, 0][:].indirect(cen_sb[:]))
+        whole_product(Y, 1, 6)
+        gate_sum(0, 0)
+        quantise(H, raw_h, nc.vector.tensor_copy, "rows0_0")
+        centres[1] = scalar_gather("centre1", rows[Y, 1], cen_sb)
+        gate_sum(0, 1)
+        whole_product(E, 1, 0)
+        whole_product(H, 0, 2)
         for d in range(D):
-            add_turned(sum0[:], term(0, d)[:], d == 0, d == D - 1)
-        gate(1, 0)
-        back0 = turn_back(sum0[:], "turned0")
-        gate(1, 1)
-        result0 = keep.tile([P, V], F32, name="result0")
-        nc.scalar.copy(result0[:], back0[:])
-        nc.sync.dma_start(out[0:P, :], result0[:])
-        gate(1, 2)
+            gate_sum(1, d)
 
-        sum1 = [sum_psum.tile([P, W], F32, name="sum1_%d" % u) for u in range(2)]
-        for d in range(D - 1):
+        turned_gate_sum(0, 2, 6)
+        message2 = turned_message(0, 2, 7)
+        gate(0, 2)
+        back0 = bank(2, "back0")
+        add_turned(back0[:], turned_term(0, 2, message2)[:], True, False)
+        sum0 = bank(1, "sum0")
+        for d in range(2):
+            gate(0, d)
+            add_turned(sum0[:], term(0, d)[:], d == 0, d == 1)
+        whole_product(H, 1, 4)
+
+        sum1 = [bank(3, "sum1_0"), bank(6, "sum1_1")]
+
+        def summed_term(d):
+            gate(1, d)
             tile = term(1, d)
             for u in range(2):
-                add_turned(sum1[u][:], tile[:, u * W : (u + 1) * W], d == 0, d == D - 2)
+                add_turned(sum1[u][:, 0:W], tile[:, u * W : (u + 1) * W], d == 0, d == D - 2)
 
+        summed_term(0)
+        turned_gate_sum(0, 3, 0)
+        summed_term(1)
+        message3 = turned_message(0, 3, 7)
+        summed_term(2)
+        gate(0, 3)
+        last_turned = turned_term(0, 3, message3)
         last = D - 1
+        gate(1, last)
+        add_turned(back0[:], to_sbuf(sum0[:], "turned0")[:], False, False)
+        add_turned(back0[:], last_turned[:], False, True)
         partial = []
-        last_gates = []
-        for u, tag in enumerate(("gate1_1", "term1_1")):
-            pre = keep.tile([P, W], F32, name="pre_last%d" % u, tag=tag)
-            nc.vector.tensor_tensor(
-                pre[:], rows[E, 1][:].indirect(entries(pos_sb[last], u * W, W)), centres[1][:, u * W : (u + 1) * W], ADD
-            )
-            half_gate = keep.tile([P, W], F32, name="last_gate%d" % u)
-            nc.scalar.activation(half_gate[:], pre[:], SIGMOID)
-            last_gates.append(half_gate)
-            partial.append(turn_back(sum1[u][:], "turned1_%d" % u))
+        for u in range(2):
+            back = bank(4 + u, "back1_%d" % u)
+            add_turned(back[:, 0:W], to_sbuf(sum1[u][:, 0:W], "turned1_%d" % u)[:], True, True)
+            partial.append(back)
+        nc.sync.dma_start(out[0:P, :], to_sbuf(back0[:], "result0")[:])
         last_terms = []
         for u in range(2):
             half_term = keep.tile([P, W], F32, name="last_term%d" % u)
             nc.vector.tensor_tensor(
-                half_term[:], rows[H, 1][:].indirect(entries(pos_sb[last], u * W, W)), last_gates[u][:], MULT
+                half_term[:],
+                rows[H, 1][:].indirect(entries(pos_sb[last], u * W, W)),
+                gates[1, last][:, u * W : (u + 1) * W],
+                MULT,
             )
             last_terms.append(half_term)
         for u in range(2):

@@ -89,14 +89,17 @@ def tile_picked_gatedg_none_p_kernel(
         codes = {}
         weight_scales = {}
 
-        def quantise(i, raw, copy, tag):
+        def round_weight(i, raw, copy, tag):
             grouped = keep.tile([P, N, PACK], BF16, name="grouped%d" % i, tag=tag, align_bytes=64)
-            code_tile = keep.tile([P, N], U32, name="codes%d" % i, align_bytes=64)
-            scale_tile = keep.tile([P, N], U8, name="weight_scales%d" % i, align_bytes=64)
             copy(
                 grouped[:].rearrange("p (c i) t -> p c t i", i=4),
                 raw[:].rearrange("p t (c i) -> p c t i", i=4),
             )
+            return grouped
+
+        def quantise(i, grouped):
+            code_tile = keep.tile([P, N], U32, name="codes%d" % i, align_bytes=64)
+            scale_tile = keep.tile([P, N], U8, name="weight_scales%d" % i, align_bytes=64)
             nc.vector.quantize_mx(
                 out=code_tile[:].bitcast(FP8X4), scales=scale_tile[:], in_=grouped[:].rearrange("p c t -> p (c t)")
             )
@@ -106,7 +109,7 @@ def tile_picked_gatedg_none_p_kernel(
 
         gathered_scales = keep.tile([P, S], U8, name="gathered_scales", align_bytes=64)
         nc.vector.tensor_copy(gathered_scales[:], scales_sb[:].indirect(offs_sb[:]))
-        quantise(Y, raw_y, nc.scalar.copy, "grouped_y")
+        quantise(Y, round_weight(Y, raw_y, nc.scalar.copy, "grouped_y"))
         node_scales = keep.tile([P, S], U8, name="node_scales", align_bytes=64)
         nc.gpsimd.memset(node_scales[:].bitcast(I32), 0)
         for r in range(ROWS_PER_QUADRANT):
@@ -122,7 +125,7 @@ def tile_picked_gatedg_none_p_kernel(
 
         pick_words(0, "picked_words0")
         pick_words(1, "raw_y", 2)
-        quantise(E, raw_e, nc.vector.tensor_copy, "words_sb")
+        quantise(E, round_weight(E, raw_e, nc.vector.tensor_copy, "words_sb"))
 
         rows = {}
 
@@ -202,63 +205,74 @@ def tile_picked_gatedg_none_p_kernel(
 
         for n in range(4):
             product(Y, 0, n * QUARTER, QUARTER, n)
+        whole_product(Y, 1, 6)
         whole_product(E, 0, 4)
         centres[0] = keep.tile([P, V], F32, name="centre0")
         nc.vector.tensor_copy(centres[0][:], rows[Y, 0][:].indirect(cen_sb[:]))
-        whole_product(Y, 1, 6)
+        grouped_h = round_weight(H, raw_h, nc.vector.tensor_copy, "rows0_0")
+        centres[1] = keep.tile([P, V], F32, name="centre1")
+        nc.vector.tensor_copy(centres[1][:, 0:W], rows[Y, 1][:].indirect(entries(cen_sb, 0, W)))
+        nc.scalar.activation(centres[1][:, W:V], rows[Y, 1][:].indirect(entries(cen_sb, W, W)), COPY)
+        quantise(H, grouped_h)
         gate_sum(0, 0)
-        quantise(H, raw_h, nc.vector.tensor_copy, "rows0_0")
-        centres[1] = scalar_gather("centre1", rows[Y, 1], cen_sb)
-        gate_sum(0, 1)
         whole_product(E, 1, 0)
         whole_product(H, 0, 2)
-        for d in range(D):
+        for d in range(1, D - 1):
+            gate_sum(0, d)
+        for d in range(2):
             gate_sum(1, d)
 
-        turned_gate_sum(0, 2, 6)
-        message2 = turned_message(0, 2, 7)
-        gate(0, 2)
-        back0 = bank(2, "back0")
-        add_turned(back0[:], turned_term(0, 2, message2)[:], True, False)
-        sum0 = bank(1, "sum0")
-        for d in range(2):
+        turned_gate_sum(0, 3, 4)
+        message0 = turned_message(0, 3, 5)
+        gate(0, 3)
+        back0 = bank(3, "back0")
+        add_turned(back0[:], turned_term(0, 3, message0)[:], True, False)
+        sum0 = bank(2, "sum0")
+
+        def summed_term0(d):
             gate(0, d)
-            add_turned(sum0[:], term(0, d)[:], d == 0, d == 1)
-        whole_product(H, 1, 4)
+            add_turned(sum0[:], term(0, d)[:], d == 0, d == D - 2)
 
-        sum1 = [bank(3, "sum1_0"), bank(6, "sum1_1")]
-
-        def summed_term(d):
+        def summed_term1(d):
             gate(1, d)
             tile = term(1, d)
             for u in range(2):
-                add_turned(sum1[u][:, 0:W], tile[:, u * W : (u + 1) * W], d == 0, d == D - 2)
+                add_turned(sum1[u][:, 0:W], tile[:, u * W : (u + 1) * W], d == 0, d == 1)
 
-        summed_term(0)
-        turned_gate_sum(0, 3, 0)
-        summed_term(1)
-        message3 = turned_message(0, 3, 7)
-        summed_term(2)
-        gate(0, 3)
-        last_turned = turned_term(0, 3, message3)
+        summed_term0(0)
+        summed_term0(1)
+        whole_product(H, 1, 6)
+        sum1 = [bank(6, "sum1_0"), bank(7, "sum1_1")]
+        summed_term0(2)
+        summed_term1(0)
+        turned_gate_sum(1, 2, 0)
+        summed_term1(1)
+        message1 = turned_message(1, 2, 1)
+        add_turned(back0[:], to_sbuf(sum0[:], "turned0")[:], False, True)
+        gate(1, 2)
+
         last = D - 1
-        gate(1, last)
-        add_turned(back0[:], to_sbuf(sum0[:], "turned0")[:], False, False)
-        add_turned(back0[:], last_turned[:], False, True)
-        partial = []
+        last_sum = keep.tile([P, V], F32, name="last_sum", tag="pre1_1")
+        last_gates = []
+        partial = [bank(4 + u, "back1_%d" % u) for u in range(2)]
         for u in range(2):
-            back = bank(4 + u, "back1_%d" % u)
-            add_turned(back[:, 0:W], to_sbuf(sum1[u][:, 0:W], "turned1_%d" % u)[:], True, True)
-            partial.append(back)
+            cols = slice(u * W, (u + 1) * W)
+            add_turned(partial[u][:, 0:W], to_sbuf(sum1[u][:, 0:W], "turned1_%d" % u)[:], True, False)
+            nc.vector.tensor_tensor(
+                last_sum[:, cols], rows[E, 1][:].indirect(entries(pos_sb[last], u * W, W)), centres[1][:, cols], ADD
+            )
+            half_gate = keep.tile([P, W], F32, name="last_gate%d" % u)
+            nc.scalar.activation(half_gate[:], last_sum[:, cols], SIGMOID)
+            last_gates.append(half_gate)
+        turned1 = turned_term(1, 2, message1)
+        for u in range(2):
+            add_turned(partial[u][:, 0:W], turned1[:, u * W : (u + 1) * W], False, True)
         nc.sync.dma_start(out[0:P, :], to_sbuf(back0[:], "result0")[:])
         last_terms = []
         for u in range(2):
             half_term = keep.tile([P, W], F32, name="last_term%d" % u)
             nc.vector.tensor_tensor(
-                half_term[:],
-                rows[H, 1][:].indirect(entries(pos_sb[last], u * W, W)),
-                gates[1, last][:, u * W : (u + 1) * W],
-                MULT,
+                half_term[:], rows[H, 1][:].indirect(entries(pos_sb[last], u * W, W)), last_gates[u][:], MULT
             )
             last_terms.append(half_term)
         for u in range(2):

@@ -36,6 +36,7 @@ def tile_picked_gatedg_none_p_kernel(
     tc, x_words, x_scales, w1, w2, w3, offs, cen, pos1, pos2, pos3, pos4, out
 ):
     nc = tc.nc
+    SHARE = V // 4
     with ExitStack() as ctx:
         keep = ctx.enter_context(tc.tile_pool(name="keep", bufs=1))
         psum = ctx.enter_context(tc.psum_pool(name="psum", bufs=1))
@@ -211,8 +212,8 @@ def tile_picked_gatedg_none_p_kernel(
         nc.vector.tensor_copy(centres[0][:], rows[Y, 0][:].indirect(cen_sb[:]))
         grouped_h = round_weight(H, raw_h, nc.vector.tensor_copy, "rows0_0")
         centres[1] = keep.tile([P, V], F32, name="centre1")
-        nc.vector.tensor_copy(centres[1][:, 0:W], rows[Y, 1][:].indirect(entries(cen_sb, 0, W)))
-        nc.scalar.activation(centres[1][:, W:V], rows[Y, 1][:].indirect(entries(cen_sb, W, W)), COPY)
+        nc.vector.tensor_copy(centres[1][:, 0:SHARE], rows[Y, 1][:].indirect(entries(cen_sb, 0, SHARE)))
+        nc.scalar.activation(centres[1][:, SHARE:V], rows[Y, 1][:].indirect(entries(cen_sb, SHARE, V - SHARE)), COPY)
         quantise(H, grouped_h)
         gate_sum(0, 0)
         whole_product(E, 1, 0)

from contextlib import ExitStack

import concourse.mybir as mybir
from concourse.masks import make_identity

K, T, S, V, N = 512, 2048, 1024, 512, 256
FLOPS = 3 * 2 * K * N * S

F32 = mybir.dt.float32
BF16 = mybir.dt.bfloat16
I32 = mybir.dt.int32
U32 = mybir.dt.uint32
U16 = mybir.dt.uint16
U8 = mybir.dt.uint8
FP8X4 = mybir.dt.float8_e4m3fn_x4
FP4X4 = mybir.dt.float4_e2m1fn_x4
ADD = mybir.AluOpType.add
MULT = mybir.AluOpType.mult
COPY = mybir.ActivationFunctionType.Copy
SIGMOID = mybir.ActivationFunctionType.Sigmoid

P = 128
QUADRANT = 32
PACK = 4
SCALE_ROWS = K // 32
ROWS_PER_QUADRANT = SCALE_ROWS * QUADRANT // P
BANK = 512
QUARTER = S // 4
BLOCKS = N // P
D = 4
W = V // 2
Y, E, H = 0, 1, 2


def tile_picked_gatedg_none_p_kernel(
    tc, x_words, x_scales, w1, w2, w3, offs, cen, pos1, pos2, pos3, pos4, out
):
    nc = tc.nc
    SHARE = V // 4
    with ExitStack() as ctx:
        keep = ctx.enter_context(tc.tile_pool(name="keep", bufs=1))
        psum = ctx.enter_context(tc.psum_pool(name="psum", bufs=1))

        def load_list(name, src):
            tile = keep.tile(list(src.shape), U16, name=name)
            nc.sync.dma_start(tile[:], src)
            return tile

        def entries(list_tile, first, count):
            return list_tile[:, first // 16 : (first + count) // 16]

        def load_weight(name, src):
            tile = keep.tile([P, PACK, N], F32, name=name, align_bytes=64)
            nc.sync.dma_start(tile[:], src.rearrange("(p j) c -> p j c", j=PACK))
            return tile

        offs_sb = load_list("offs_sb", offs)
        scales_sb = keep.tile([P, T], U8, name="scales_sb")
        nc.scalar.dma_start(scales_sb[P - SCALE_ROWS : P, :].bitcast(I32), x_scales[0].bitcast(I32))
        nc.vector.memset(scales_sb[0 : P - SCALE_ROWS, :].bitcast(I32), 0)

        raw_y = keep.tile([P, PACK, N], F32, name="raw_y", align_bytes=64)
        w1_rows = w1.rearrange("(p j) c -> p j c", j=PACK)
        nc.sync.dma_start(raw_y[:, 0:2, :], w1_rows[:, 0:2, :])
        nc.scalar.dma_start(raw_y[:, 2:4, :], w1_rows[:, 2:4, :])
        words_sb = keep.tile([P, T], U16, name="words_sb", align_bytes=64)
        nc.sync.dma_start(words_sb[:].bitcast(I32), x_words[0].bitcast(I32))
        raw_e = keep.tile([P, PACK, N], F32, name="raw_e", align_bytes=64)
        w2_rows = w2.rearrange("(p j) c -> p j c", j=PACK)
        nc.sync.dma_start(raw_e[:, 0:2, :], w2_rows[:, 0:2, :])

        ident = keep.tile([P, P], F32, name="ident")
        make_identity(nc, ident[:])
        warm = keep.tile([P, 1], F32, name="warm")
        zero = keep.tile([P, 1], F32, name="zero")
        nc.vector.memset(zero[:], 0.0)
        nc.scalar.activation(warm[:], zero[:], SIGMOID)

        picked_words = {}

        def pick_words(half, tag, pieces=1):
            tile = keep.tile([P, BANK], U16, name="picked_words%d" % half, tag=tag, align_bytes=64)
            width = BANK // pieces
            for first in range(0, BANK, width):
                nc.vector.tensor_copy(
                    tile[:, first : first + width], words_sb[:].indirect(entries(offs_sb, half * BANK + first, width))
                )
            picked_words[half] = tile

        codes = {}
        weight_scales = {}

        def round_weight(i, raw, copy, tag):
            grouped = keep.tile([P, N, PACK], BF16, name="grouped%d" % i, tag=tag, align_bytes=64)
            copy(
                grouped[:].rearrange("p (c i) t -> p c t i", i=4),
                raw[:].rearrange("p t (c i) -> p c t i", i=4),
            )
            return grouped

        def quantise(i, grouped):
            code_tile = keep.tile([P, N], U32, name="codes%d" % i, align_bytes=64)
            scale_tile = keep.tile([P, N], U8, name="weight_scales%d" % i, align_bytes=64)
            nc.vector.quantize_mx(
                out=code_tile[:].bitcast(FP8X4), scales=scale_tile[:], in_=grouped[:].rearrange("p c t -> p (c t)")
            )
            for b in range(BLOCKS):
                codes[i, b] = code_tile[:, b * P : (b + 1) * P]
                weight_scales[i, b] = scale_tile[:, b * P : (b + 1) * P]

        gathered_scales = keep.tile([P, S], U8, name="gathered_scales", align_bytes=64)
        nc.vector.tensor_copy(gathered_scales[:], scales_sb[:].indirect(offs_sb[:]))
        quantise(Y, round_weight(Y, raw_y, nc.scalar.copy, "grouped_y"))
        node_scales = keep.tile([P, S], U8, name="node_scales", align_bytes=64)
        nc.gpsimd.memset(node_scales[:].bitcast(I32), 0)
        for r in range(ROWS_PER_QUADRANT):
            queue = nc.sync if r < 2 else nc.scalar
            queue.dma_start(
                node_scales[r:P:QUADRANT, :].bitcast(I32),
                gathered_scales[P - SCALE_ROWS + r : P : ROWS_PER_QUADRANT, :].bitcast(I32),
            )
        nc.sync.dma_start(raw_e[:, 2:4, :], w2_rows[:, 2:4, :])
        cen_sb = load_list("cen_sb", cen)
        raw_h = load_weight("raw_h", w3)
        pos_sb = [load_list("pos_sb%d" % n, src) for n, src in enumerate((pos1, pos2, pos3, pos4))]

        pick_words(0, "picked_words0")
        pick_words(1, "raw_y", 2)
        quantise(E, round_weight(E, raw_e, nc.vector.tensor_copy, "words_sb"))

        rows = {}

        def bank(number, name):
            return psum.tile([P, BANK], F32, name=name, tag="bank%d" % number)

        def product(i, b, first, width, number, copy=nc.scalar.copy):
            acc = bank(number, "acc%d_%d_%d" % (i, b, first))
            half, start = divmod(first, BANK)
            nc.tensor.matmul_mx(
                out=acc[:, 0:width],
                lhsT=codes[i, b].bitcast(FP8X4),
                lhsT_scale=weight_scales[i, b],
                rhs=picked_words[half][:, start : start + width].bitcast(FP4X4),
                rhs_scale=node_scales[:, first : first + width],
                start=True,
                stop=True,
            )
            if (i, b) not in rows:
                rows[i, b] = keep.tile([P, S], F32, name="rows%d_%d" % (i, b), align_bytes=64)
            copy(rows[i, b][:, first : first + width], acc[:, 0:width])

        def whole_product(i, b, number):
            for half in range(2):
                product(i, b, half * BANK, BANK, number + half)

        def scalar_gather(name, window, list_tile):
            tile = keep.tile([P, V], F32, name=name)
            nc.scalar.activation(tile[:], window[:].indirect(list_tile[:]), COPY)
            return tile

        def add_turned(total, src, opens, closes):
            chunks = src.shape[1] // P
            for c in range(chunks):
                cols = slice(c * P, (c + 1) * P)
                nc.tensor.matmul(
                    total[:, cols], src[:, cols], ident[:], is_transpose=True,
                    start=(opens and c == 0), stop=(closes and c == chunks - 1),
                )

        centres = {}
        sums = {}
        gates = {}

        def gate_sum(b, d):
            sums[b, d] = keep.tile([P, V], F32, name="pre%d_%d" % (b, d))
            nc.vector.tensor_tensor(sums[b, d][:], rows[E, b][:].indirect(pos_sb[d][:]), centres[b][:], ADD)

        def gate(b, d):
            gates[b, d] = keep.tile([P, V], F32, name="gate%d_%d" % (b, d))
            nc.scalar.activation(gates[b, d][:], sums[b, d][:], SIGMOID)

        def term(b, d):
            tile = keep.tile([P, V], F32, name="term%d_%d" % (b, d))
            nc.vector.tensor_tensor(tile[:], rows[H, b][:].indirect(pos_sb[d][:]), gates[b, d][:], MULT)
            return tile

        def turned_gate_sum(b, d, number):
            sums[b, d] = bank(number, "pre%d_%d" % (b, d))
            add_turned(sums[b, d][:], centres[b][:], True, False)
            add_turned(sums[b, d][:], scalar_gather("e_picked%d_%d" % (b, d), rows[E, b], pos_sb[d])[:], False, True)

        def turned_message(b, d, number):
            turned = bank(number, "message%d_%d" % (b, d))
            add_turned(turned[:], scalar_gather("h_picked%d_%d" % (b, d), rows[H, b], pos_sb[d])[:], True, True)
            return turned

        def turned_term(b, d, message):
            tile = keep.tile([P, V], F32, name="term%d_%d" % (b, d))
            nc.vector.tensor_tensor(tile[:], message[:], gates[b, d][:], MULT)
            return tile

        def to_sbuf(total, name):
            tile = keep.tile([P, total.shape[1]], F32, name=name)
            nc.scalar.copy(tile[:], total)
            return tile

        for n in range(4):
            product(Y, 0, n * QUARTER, QUARTER, n)
        whole_product(Y, 1, 6)
        whole_product(E, 0, 4)
        centres[0] = keep.tile([P, V], F32, name="centre0")
        nc.vector.tensor_copy(centres[0][:], rows[Y, 0][:].indirect(cen_sb[:]))
        grouped_h = round_weight(H, raw_h, nc.vector.tensor_copy, "rows0_0")
        centres[1] = keep.tile([P, V], F32, name="centre1")
        nc.vector.tensor_copy(centres[1][:, 0:SHARE], rows[Y, 1][:].indirect(entries(cen_sb, 0, SHARE)))
        nc.scalar.activation(centres[1][:, SHARE:V], rows[Y, 1][:].indirect(entries(cen_sb, SHARE, V - SHARE)), COPY)
        quantise(H, grouped_h)
        gate_sum(0, 0)
        whole_product(E, 1, 0)
        whole_product(H, 0, 2)
        for d in range(1, D - 1):
            gate_sum(0, d)
        for d in range(2):
            gate_sum(1, d)

        turned_gate_sum(0, 3, 4)
        message0 = turned_message(0, 3, 5)
        gate(0, 3)
        back0 = bank(3, "back0")
        add_turned(back0[:], turned_term(0, 3, message0)[:], True, False)
        sum0 = bank(2, "sum0")

        def summed_term0(d):
            gate(0, d)
            add_turned(sum0[:], term(0, d)[:], d == 0, d == D - 2)

        def summed_term1(d):
            gate(1, d)
            tile = term(1, d)
            for u in range(2):
                add_turned(sum1[u][:, 0:W], tile[:, u * W : (u + 1) * W], d == 0, d == 1)

        summed_term0(0)
        summed_term0(1)
        whole_product(H, 1, 6)
        sum1 = [bank(6, "sum1_0"), bank(7, "sum1_1")]
        summed_term0(2)
        summed_term1(0)
        turned_gate_sum(1, 2, 0)
        summed_term1(1)
        message1 = turned_message(1, 2, 1)
        add_turned(back0[:], to_sbuf(sum0[:], "turned0")[:], False, True)
        gate(1, 2)

        last = D - 1
        last_sum = keep.tile([P, V], F32, name="last_sum", tag="pre1_1")
        last_gates = []
        partial = [bank(4 + u, "back1_%d" % u) for u in range(2)]
        for u in range(2):
            cols = slice(u * W, (u + 1) * W)
            add_turned(partial[u][:, 0:W], to_sbuf(sum1[u][:, 0:W], "turned1_%d" % u)[:], True, False)
            nc.vector.tensor_tensor(
                last_sum[:, cols], rows[E, 1][:].indirect(entries(pos_sb[last], u * W, W)), centres[1][:, cols], ADD
            )
            half_gate = keep.tile([P, W], F32, name="last_gate%d" % u)
            nc.scalar.activation(half_gate[:], last_sum[:, cols], SIGMOID)
            last_gates.append(half_gate)
        turned1 = turned_term(1, 2, message1)
        for u in range(2):
            add_turned(partial[u][:, 0:W], turned1[:, u * W : (u + 1) * W], False, True)
        nc.sync.dma_start(out[0:P, :], to_sbuf(back0[:], "result0")[:])
        last_terms = []
        for u in range(2):
            half_term = keep.tile([P, W], F32, name="last_term%d" % u)
            nc.vector.tensor_tensor(
                half_term[:], rows[H, 1][:].indirect(entries(pos_sb[last], u * W, W)), last_gates[u][:], MULT
            )
            last_terms.append(half_term)
        for u in range(2):
            result1 = keep.tile([P, W], F32, name="result1_%d" % u)
            nc.vector.tensor_tensor(result1[:], partial[u][:, 0:W], last_terms[u][:], ADD)
            nc.sync.dma_start(out[P : 2 * P, u * W : (u + 1) * W], result1[:])
